import numpy as np
import ml_dtypes


def mxq(x, axis, fmt="e4m3"):
    dtype, down = {"e4m3": (ml_dtypes.float8_e4m3fn, 7), "e5m2": (ml_dtypes.float8_e5m2, 14)}[fmt]
    v = np.moveaxis(np.asarray(x, np.float32).astype(ml_dtypes.bfloat16).astype(np.float64), axis, -1)
    blocks = v.reshape(v.shape[:-1] + (-1, 32))
    amax = np.abs(blocks).max(-1, keepdims=True)
    byte = np.maximum(np.where(amax > 0, np.frexp(amax)[1] - 1 + 127, 0) - down, 1)
    scale = np.exp2(byte - 127.0)
    codes = (blocks / scale).astype(np.float32).astype(dtype).astype(np.float64)
    return np.moveaxis((codes * scale).reshape(v.shape), -1, axis)


WIDE = False


def mx_kscale(k):
    if not WIDE:
        return np.ones(k)
    levels = np.array([10, -10, 5, -5, 0])
    if k % 512:
        return np.exp2(np.random.permutation(np.resize(levels, k // 32))).repeat(32)
    a = np.empty((k // 512, 16))
    for p in range(k // 512):
        a[p, :8] = np.random.permutation(np.resize(levels, 8))
        for g in range(8):
            far = levels[np.abs(levels - a[p, g]) >= 10]
            a[p, g + 8] = far[np.random.randint(len(far))]
    return np.exp2(a.ravel()).repeat(32)


def f64(x):
    return np.asarray(x).astype(np.float64)


def striped(idx):
    return np.tile(idx.reshape(-1, 16).T, (8, 1)).astype(np.uint16)


def unstriped(offs):
    return offs[:16].T.reshape(-1).astype(np.int64)


E2M1 = np.array([0.0, 0.5, 1.0, 1.5, 2.0, 3.0, 4.0, 6.0, -0.0, -0.5, -1.0, -1.5, -2.0, -3.0, -4.0, -6.0])


def pack_weight(w, fmt):
    k, n = w.shape
    w = f64(np.asarray(w, np.float32).astype(ml_dtypes.bfloat16)).reshape(k // 32, 32, n)
    amax = np.abs(w).max(1)
    if fmt == "e4m3":
        byte = np.frexp(amax)[1] - 1 + 127 - 7
    else:
        mant, ex = np.frexp(amax / 6.0)
        byte = np.where(mant > 0.5, ex, ex - 1) + 127
    byte = np.clip(np.where(amax > 0, byte, 1), 1, 254)
    scaled = (w * np.exp2(127.0 - byte)[:, None, :]).reshape(k, n).astype(np.float32)
    by_word = np.ascontiguousarray(scaled.reshape(k // 512, 128, 4, n).transpose(0, 1, 3, 2))
    if fmt == "e4m3":
        words = by_word.astype(ml_dtypes.float8_e4m3fn).view(np.uint8)
    else:
        c = by_word.astype(ml_dtypes.float4_e2m1fn).view(np.uint8) & 0xF
        words = (c[..., 0::2] | (c[..., 1::2] << 4)).reshape(k // 512, 128, 2 * n)
    return np.ascontiguousarray(words), np.ascontiguousarray(byte.astype(np.uint8).reshape(k // 512, 16, n))


def unpack_weight(words, scales, fmt):
    g, _, n = scales.shape
    words = np.ascontiguousarray(words).reshape(g, 128, n, -1)
    if fmt == "e4m3":
        vals = words.view(ml_dtypes.float8_e4m3fn).astype(np.float64)
    else:
        nib = np.empty((g, 128, n, 4), np.uint8)
        nib[..., 0::2] = words & 0xF
        nib[..., 1::2] = words >> 4
        vals = E2M1[nib]
    vals = vals * np.repeat(np.exp2(scales.astype(np.float64) - 127.0), 8, axis=1)[..., None]
    return vals.transpose(0, 1, 3, 2).reshape(g * 512, n)


def gelu(v):
    return 0.5 * v * (1.0 + np.tanh(np.sqrt(2.0 / np.pi) * (v + 0.044715 * v**3)))


K, H, T, S, T2, P = 1536, 512, 2048, 1024, 2048, 512

def setup_inputs():
    n = np.random.standard_normal
    s = mx_kscale(K)[:, None]
    u = mx_kscale(H)[:, None]
    tab_words, tab_scales = pack_weight(n((K, T)) * s, "e4m3")
    w4_words, w4_scales = pack_weight(0.55 * n((K, H)) / np.sqrt(K) / s, "e2m1")
    return {
        "tab_words": tab_words, "tab_scales": tab_scales,
        "offs": striped(np.random.permutation(T)[:S]),
        "offs2": striped(np.random.permutation(T2)[:S]),
        "offs3": striped(np.random.permutation(T2)[:P]),
        "offs4": striped(np.random.permutation(T2)[:P]),
        "w1": (n((K, H)) / np.sqrt(K) / s * u.T).astype(np.float32),
        "w4_words": w4_words, "w4_scales": w4_scales,
        "wgs": np.exp(0.3 * n((128, S))).astype(np.float32),
        "page0": (n((H, T2)) * u).astype(np.float32),
        "mu": ((0.35 + 0.3 * n(H)) * u[:, 0]).astype(np.float32),
        "gain": (n(H) / np.sqrt(H) / u[:, 0] ** 2).astype(np.float32),
        "bvec": (0.7 * n(P)).astype(np.float32),
    }

def reference(tab_words, tab_scales, offs, offs2, offs3, offs4, w1, w4_words, w4_scales, wgs, page0, mu, gain, bvec):
    v = unpack_weight(tab_words, tab_scales, "e4m3")[:, unstriped(offs)]
    w4 = unpack_weight(w4_words, w4_scales, "e2m1")
    a = mxq(f64(w1), 0, "e4m3").T @ v
    b = w4.T @ v
    h = np.abs(a) * np.cos(b)
    page = f64(page0).copy()
    page[:, unstriped(offs2)] = np.tile(f64(wgs), (H // 128, 1)) * h
    x1 = page[:, unstriped(offs3)] - f64(mu)[:, None]
    x2 = np.abs(page[:, unstriped(offs4)]) * f64(gain)[:, None]
    e = mxq(x1, 0, "e4m3").T @ mxq(x2, 0, "e4m3")
    return e + f64(bvec)[:, None]

@@ -1,0 +1,271 @@
+import math
+from contextlib import ExitStack
+
+import concourse.mybir as mybir
+
+K, H, T, S, T2, M = 1536, 512, 2048, 1024, 2048, 512
+FLOPS = 2 * (2 * K * H * S + H * M * M)
+
+F32 = mybir.dt.float32
+BF16 = mybir.dt.bfloat16
+I32 = mybir.dt.int32
+U32 = mybir.dt.uint32
+U16 = mybir.dt.uint16
+U8 = mybir.dt.uint8
+E4M3X4 = mybir.dt.float8_e4m3fn_x4
+E2M1X4 = mybir.dt.float4_e2m1fn_x4
+ACT = mybir.ActivationFunctionType
+ALU = mybir.AluOpType
+
+P = 128
+PACK = 4
+PASSES = K // (P * PACK)
+HALF = 512
+HALVES = S // HALF
+TWO_PI = 2.0 * math.pi
+
+
+def tile_list_calciner_batch_likeness_kernel(
+    tc, tab_words, tab_scales, offs, offs2, offs3, offs4, w1, w4_words, w4_scales, wgs, page0, mu, gain, bvec, out
+):
+    nc = tc.nc
+    with ExitStack() as ctx:
+        lists = ctx.enter_context(tc.tile_pool(name="lists", bufs=1))
+        keep = ctx.enter_context(tc.tile_pool(name="keep", bufs=1))
+        work = ctx.enter_context(tc.tile_pool(name="work", bufs=3))
+        psum = ctx.enter_context(tc.psum_pool(name="psum", bufs=4))
+
+        idx = lists.tile([P, S // 16], U16, name="idx")
+        idx2 = lists.tile([P, S // 16], U16, name="idx2")
+        idx3 = lists.tile([P, M // 16], U16, name="idx3")
+        idx4 = lists.tile([P, M // 16], U16, name="idx4")
+
+        tsc = keep.tile([P, T], U8, name="tsc", align_bytes=64)
+        w4s_raw = keep.tile([P, PASSES, H], U8, name="w4s_raw", align_bytes=64)
+        moved = [keep.tile([P, S], U8, name=f"moved{a}", align_bytes=64) for a in range(1, PASSES)]
+        nc.vector.memset(tsc[:].bitcast(I32), 0)
+        nc.vector.memset(w4s_raw[:].rearrange("p a c -> p (a c)").bitcast(I32), 0)
+        for plane in moved:
+            nc.vector.memset(plane[:].bitcast(I32), 0)
+
+        nc.sync.dma_start(idx[:], offs)
+        w4_raw = keep.tile([P, PASSES, 2 * H], U8, name="w4_raw", align_bytes=64)
+        nc.sync.dma_start(w4_raw[:].bitcast(I32), w4_words.rearrange("a p n -> p a n").bitcast(I32))
+        for q in range(4):
+            nc.gpsimd.dma_start(
+                tsc[32 * q : 32 * q + 4 * PASSES, :].bitcast(I32), tab_scales[:, 4 * q : 4 * q + 4, :].bitcast(I32)
+            )
+        for q in range(4):
+            nc.gpsimd.dma_start(
+                w4s_raw[32 * q : 32 * q + 4, :, :].bitcast(I32),
+                w4_scales[:, 4 * q : 4 * q + 4, :].rearrange("a r c -> r a c").bitcast(I32),
+            )
+        tw = [keep.tile([P, T], I32, name=f"tw{a}") for a in range(PASSES)]
+        w1_raw = [keep.tile([P, PACK, H], F32, name=f"w1_raw{a}") for a in range(PASSES)]
+
+        def load_w1(a):
+            nc.sync.dma_start(w1_raw[a][:], w1[512 * a : 512 * (a + 1), :].rearrange("(p j) c -> p j c", j=PACK))
+
+        for a in range(PASSES - 1):
+            load_w1(a)
+        for a in range(PASSES):
+            nc.sync.dma_start(tw[a][:], tab_words[a].rearrange("p t i -> p (t i)").bitcast(I32))
+        load_w1(PASSES - 1)
+        wg = [keep.tile([P, S], F32, name=f"wg{t}") for t in range(PACK)]
+        page = [keep.tile([P, T2], F32, name=f"page{t}") for t in range(PACK)]
+        wgs_rows = wgs.rearrange("(q t) s -> t q s", t=PACK)
+        page_rows = page0.rearrange("(p t) c -> t p c", t=PACK)
+        mu_sb = keep.tile([P, PACK], F32, name="mu_sb")
+        gain_sb = keep.tile([P, PACK], F32, name="gain_sb")
+        bvec_sb = keep.tile([P, M // P], F32, name="bvec_sb")
+        for t in range(PACK):
+            if t == 0:
+                nc.sync.dma_start(idx2[:], offs2)
+            nc.sync.dma_start(page[t][:], page_rows[t])
+            for q in range(4):
+                nc.sync.dma_start(wg[t][32 * q : 32 * q + 32, :], wgs_rows[t])
+            if t == 0:
+                nc.sync.dma_start(idx4[:], offs4)
+                nc.sync.dma_start(idx3[:], offs3)
+                nc.sync.dma_start(mu_sb[:], mu.rearrange("(p t) -> p t", t=PACK))
+                nc.sync.dma_start(gain_sb[:], gain.rearrange("(p t) -> p t", t=PACK))
+        with nc.allow_non_contiguous_dma(reason="one offset to a partition"):
+            nc.sync.dma_start(bvec_sb[:], bvec.rearrange("(b p) -> p b", p=P))
+
+        w4_c = keep.tile([P, PASSES, PACK, P], U16, name="w4_c", align_bytes=64)
+        w4_s = keep.tile([P, PASSES, PACK, P], U8, name="w4_s", align_bytes=64)
+        nc.vector.tensor_copy(w4_c[:], w4_raw[:].bitcast(U16).rearrange("p a (q t) -> p a t q", t=PACK))
+        nc.vector.tensor_copy(w4_s[:], w4s_raw[:].rearrange("p a (q t) -> p a t q", t=PACK))
+
+        gsc = keep.tile([P, S], U8, name="gsc", align_bytes=64)
+        nc.vector.tensor_copy(gsc[:], tsc[:].indirect(idx[:]))
+        for a in range(1, PASSES):
+            nc.gpsimd.dma_start(moved[a - 1][0:112, :].bitcast(I32), gsc[4 * a : 4 * a + 112, :].bitcast(I32))
+        planes = [gsc] + moved
+        w1_c, w1_s = {}, {}
+
+        def quantise_w1(a, t0, n, copy):
+            grouped = keep.tile([P, n, P, PACK], BF16, name=f"w1_b{a}_{t0}", align_bytes=64)
+            src = w1_raw[a][:].rearrange("p j (q t) -> p q j t", t=PACK)[:, :, :, t0 : t0 + n]
+            copy(grouped[:].rearrange("p t q j -> p q j t"), src)
+            codes = keep.tile([P, n, P], U32, name=f"w1_c{a}_{t0}", align_bytes=64)
+            scales = keep.tile([P, n, P], U8, name=f"w1_s{a}_{t0}", align_bytes=64)
+            nc.vector.quantize_mx(
+                codes[:].rearrange("p t q -> p (t q)").bitcast(E4M3X4),
+                scales[:].rearrange("p t q -> p (t q)"),
+                grouped[:].rearrange("p t q j -> p (t q j)"),
+            )
+            for t in range(n):
+                w1_c[a, t0 + t] = codes[:, t, :]
+                w1_s[a, t0 + t] = scales[:, t, :]
+
+        for a in range(PASSES - 1):
+            quantise_w1(a, 0, PACK, nc.scalar.copy)
+        gw = {}
+        for a in range(PASSES):
+            for hf in range(HALVES):
+                gw[a, hf] = keep.tile([P, HALF], U32, name=f"gw{a}_{hf}", align_bytes=64)
+                nc.vector.tensor_copy(gw[a, hf][:], tw[a][:].bitcast(U32).indirect(idx[:, 32 * hf : 32 * hf + 32]))
+        quantise_w1(PASSES - 1, 0, 2, nc.vector.tensor_copy)
+
+        size, rest, cos_b, abs_a, picked = {}, {}, {}, {}, {}
+
+        def product(acc, codes, scales, hf):
+            for a in range(PASSES):
+                nc.tensor.matmul_mx(
+                    acc[:],
+                    lhsT=codes[a],
+                    lhsT_scale=scales[a],
+                    rhs=gw[a, hf][:].bitcast(E4M3X4),
+                    rhs_scale=planes[a][:, HALF * hf : HALF * (hf + 1)],
+                    start=(a == 0),
+                    stop=(a == PASSES - 1),
+                )
+
+        def reduce_angles(t, hf):
+            acc = psum.tile([P, HALF], F32, name="acc_b", tag="acc_b")
+            product(
+                acc,
+                [w4_c[:, a, t, :].bitcast(E2M1X4) for a in range(PASSES)],
+                [w4_s[:, a, t, :] for a in range(PASSES)],
+                hf,
+            )
+            size[t, hf] = work.tile([P, HALF], F32, name="size", bufs=4)
+            nc.scalar.activation(size[t, hf][:], acc[:], ACT.Abs)
+            turns = work.tile([P, HALF], U32, name="turns")
+            nc.scalar.activation(turns[:], acc[:], ACT.Abs, scale=1.0 / TWO_PI)
+            rest[t, hf] = work.tile([P, HALF], F32, name="rest")
+            nc.vector.scalar_tensor_tensor(
+                rest[t, hf][:], turns[:].bitcast(I32), -TWO_PI, size[t, hf][:], ALU.mult, ALU.add
+            )
+
+        def cosine(t, hf):
+            folded = work.tile([P, HALF], F32, name="folded", bufs=2)
+            nc.scalar.activation(folded[:], rest[t, hf][:], ACT.Abs)
+            cos_b[t, hf] = work.tile([P, HALF], F32, name="cos_b")
+            nc.scalar.activation(cos_b[t, hf][:], folded[:], ACT.Sin, bias=math.pi / 2, scale=-1.0)
+
+        def magnitudes(t, hf):
+            acc = psum.tile([P, HALF], F32, name="acc_a", tag="acc_a")
+            product(
+                acc,
+                [w1_c[a, t].bitcast(E4M3X4) for a in range(PASSES)],
+                [w1_s[a, t] for a in range(PASSES)],
+                hf,
+            )
+            abs_a[t, hf] = work.tile([P, HALF], F32, name="abs_a")
+            nc.scalar.activation(abs_a[t, hf][:], acc[:], ACT.Abs)
+
+        def refresh(t, hf):
+            if hf == 1 and t + 1 < PACK:
+                h = size[t + 1, 1]
+            else:
+                h = work.tile([P, HALF], F32, name="h", bufs=2)
+            nc.vector.tensor_tensor(h[:], abs_a[t, hf][:], cos_b[t, hf][:], ALU.mult)
+            nc.vector.tensor_tensor(
+                page[t][:].indirect(idx2[:, 32 * hf : 32 * hf + 32]),
+                h[:],
+                wg[t][:, HALF * hf : HALF * (hf + 1)],
+                ALU.mult,
+            )
+
+        neg_mu = keep.tile([P, PACK], F32, name="neg_mu")
+        nc.vector.tensor_scalar(neg_mu[:], mu_sb[:], -1.0, None, ALU.mult)
+        x1_b = keep.tile([P, M, PACK], BF16, name="x1_b", align_bytes=64)
+        x2_b = keep.tile([P, M, PACK], BF16, name="x2_b", align_bytes=64)
+
+        def pick(t):
+            for name, lst in (("ref", idx4), ("new", idx3)):
+                picked[name, t] = work.tile([P, M], F32, name="picked", bufs=6)
+                nc.vector.tensor_copy(picked[name, t][:], page[t][:].indirect(lst[:]))
+
+        def reference_rows(t):
+            size2 = work.tile([P, M], F32, name="size2", bufs=2)
+            nc.scalar.activation(size2[:], picked["ref", t][:], ACT.Abs)
+            nc.scalar.activation(x2_b[:, :, t], size2[:], ACT.Copy, scale=gain_sb[:, t : t + 1])
+
+        def new_rows(t):
+            if t < 2:
+                nc.scalar.activation(x1_b[:, :, t], picked["new", t][:], ACT.Identity, bias=neg_mu[:, t : t + 1])
+            else:
+                nc.vector.tensor_scalar(x1_b[:, :, t], picked["new", t][:], mu_sb[:, t : t + 1], None, ALU.subtract)
+
+        for hf in range(HALVES):
+            reduce_angles(0, hf)
+        for hf in range(HALVES):
+            cosine(0, hf)
+            magnitudes(0, hf)
+            if hf == 0:
+                refresh(0, 0)
+        for t in range(PACK):
+            more = t + 1 < PACK
+            if more:
+                for hf in range(HALVES):
+                    reduce_angles(t + 1, hf)
+            if t == 0:
+                quantise_w1(PASSES - 1, 2, 2, nc.scalar.copy)
+            else:
+                reference_rows(t - 1)
+            refresh(t, 1)
+            pick(t)
+            if more:
+                for hf in range(HALVES):
+                    cosine(t + 1, hf)
+                for hf in range(HALVES):
+                    magnitudes(t + 1, hf)
+            if t in (1, 2):
+                new_rows(t - 1)
+            if t >= 2:
+                new_rows(t)
+            if more:
+                refresh(t + 1, 0)
+        reference_rows(PACK - 1)
+
+        x1_c = keep.tile([P, M], U32, name="x1_c", align_bytes=64)
+        x1_s = keep.tile([P, M], U8, name="x1_s", align_bytes=64)
+        x2_c = keep.tile([P, M], U32, name="x2_c", align_bytes=64)
+        x2_s = keep.tile([P, M], U8, name="x2_s", align_bytes=64)
+        nc.vector.quantize_mx(x2_c[:].bitcast(E4M3X4), x2_s[:], x2_b[:].rearrange("p m t -> p (m t)"))
+        for b in range(M // P):
+            rows = slice(P * b, P * (b + 1))
+            nc.vector.quantize_mx(
+                x1_c[:, rows].bitcast(E4M3X4), x1_s[:, rows], x1_b[:, rows, :].rearrange("p m t -> p (m t)")
+            )
+        for b in range(M // P):
+            rows = slice(P * b, P * (b + 1))
+            acc = psum.tile([P, M], F32, name="acc_e", tag=("acc_a", "acc_b")[b % 2])
+            nc.tensor.matmul_mx(
+                acc[:],
+                lhsT=x1_c[:, rows].bitcast(E4M3X4),
+                lhsT_scale=x1_s[:, rows],
+                rhs=x2_c[:].bitcast(E4M3X4),
+                rhs_scale=x2_s[:],
+                start=True,
+                stop=True,
+            )
+            res = work.tile([P, M], F32, name="res", tag="picked", bufs=6)
+            if b % 2 == 0:
+                nc.scalar.activation(res[:], acc[:], ACT.Identity, bias=bvec_sb[:, b : b + 1])
+            else:
+                nc.vector.tensor_scalar(res[:], acc[:], bvec_sb[:, b : b + 1], None, ALU.add)
+            nc.sync.dma_start(out[rows, :], res[:])

@@ -48,64 +48,70 @@ def tile_list_calciner_batch_likeness_kernel(
         for plane in moved:
             nc.vector.memset(plane[:].bitcast(I32), 0)
 
-        nc.sync.dma_start(idx[:], offs)
-        w4_raw = keep.tile([P, PASSES, 2 * H], U8, name="w4_raw", align_bytes=64)
-        nc.sync.dma_start(w4_raw[:].bitcast(I32), w4_words.rearrange("a p n -> p a n").bitcast(I32))
-        for q in range(4):
-            nc.gpsimd.dma_start(
-                tsc[32 * q : 32 * q + 4 * PASSES, :].bitcast(I32), tab_scales[:, 4 * q : 4 * q + 4, :].bitcast(I32)
-            )
-        for q in range(4):
-            nc.gpsimd.dma_start(
-                w4s_raw[32 * q : 32 * q + 4, :, :].bitcast(I32),
-                w4_scales[:, 4 * q : 4 * q + 4, :].rearrange("a r c -> r a c").bitcast(I32),
-            )
-        tw = [keep.tile([P, T], I32, name=f"tw{a}") for a in range(PASSES)]
-        w1_raw = [keep.tile([P, PACK, H], F32, name=f"w1_raw{a}") for a in range(PASSES)]
+        w1_raw, tw, wg, page = {}, {}, {}, {}
+        wgs_rows = wgs.rearrange("(q t) s -> t q s", t=PACK)
+        page_rows = page0.rearrange("(p t) c -> t p c", t=PACK)
 
         def load_w1(a):
+            w1_raw[a] = keep.tile([P, PACK, H], F32, name=f"w1_raw{a}", tag=f"w1_stage{a % 2}", align_bytes=64)
             nc.sync.dma_start(w1_raw[a][:], w1[512 * a : 512 * (a + 1), :].rearrange("(p j) c -> p j c", j=PACK))
 
+        def load_page(t):
+            page[t] = keep.tile(
+                [P, T2], F32, name=f"page{t}", tag=("w1_stage1", "table2", "w1_stage0", "rounded0")[t], align_bytes=64
+            )
+            nc.sync.dma_start(page[t][:], page_rows[t])
+
+        def load_wgs(t):
+            wg[t] = keep.tile([P, S], F32, name=f"wg{t}", tag=f"rounded{(0, 1, 3, 1)[t]}", align_bytes=64)
+            for q in range(4):
+                nc.sync.dma_start(wg[t][32 * q : 32 * q + 32, :], wgs_rows[t])
+
+        w4_raw = keep.tile([P, PASSES, 2 * H], U8, name="w4_raw", align_bytes=64)
+        nc.sync.dma_start(w4_raw[:].bitcast(I32), w4_words.rearrange("a p n -> p a n").bitcast(I32))
+        nc.sync.dma_start(idx[:], offs)
+        nc.sync.dma_start(idx2[:], offs2)
+        nc.sync.dma_start(idx4[:], offs4)
+        nc.sync.dma_start(idx3[:], offs3)
         for a in range(PASSES - 1):
             load_w1(a)
         for a in range(PASSES):
+            tw[a] = keep.tile([P, T], I32, name=f"tw{a}", tag=f"table{a}", align_bytes=64)
             nc.sync.dma_start(tw[a][:], tab_words[a].rearrange("p t i -> p (t i)").bitcast(I32))
-        load_w1(PASSES - 1)
-        wg = [keep.tile([P, S], F32, name=f"wg{t}") for t in range(PACK)]
-        page = [keep.tile([P, T2], F32, name=f"page{t}") for t in range(PACK)]
-        wgs_rows = wgs.rearrange("(q t) s -> t q s", t=PACK)
-        page_rows = page0.rearrange("(p t) c -> t p c", t=PACK)
+        for q in range(4):
+            nc.scalar.dma_start(
+                tsc[32 * q : 32 * q + 4 * PASSES, :].bitcast(I32), tab_scales[:, 4 * q : 4 * q + 4, :].bitcast(I32)
+            )
+        for q in range(4):
+            nc.scalar.dma_start(
+                w4s_raw[32 * q : 32 * q + 4, :, :].bitcast(I32),
+                w4_scales[:, 4 * q : 4 * q + 4, :].rearrange("a r c -> r a c").bitcast(I32),
+            )
         mu_sb = keep.tile([P, PACK], F32, name="mu_sb")
         gain_sb = keep.tile([P, PACK], F32, name="gain_sb")
         bvec_sb = keep.tile([P, M // P], F32, name="bvec_sb")
-        for t in range(PACK):
-            if t == 0:
-                nc.sync.dma_start(idx2[:], offs2)
-            nc.sync.dma_start(page[t][:], page_rows[t])
-            for q in range(4):
-                nc.sync.dma_start(wg[t][32 * q : 32 * q + 32, :], wgs_rows[t])
-            if t == 0:
-                nc.sync.dma_start(idx4[:], offs4)
-                nc.sync.dma_start(idx3[:], offs3)
-                nc.sync.dma_start(mu_sb[:], mu.rearrange("(p t) -> p t", t=PACK))
-                nc.sync.dma_start(gain_sb[:], gain.rearrange("(p t) -> p t", t=PACK))
+        nc.gpsimd.dma_start(mu_sb[:], mu.rearrange("(p t) -> p t", t=PACK))
+        nc.gpsimd.dma_start(gain_sb[:], gain.rearrange("(p t) -> p t", t=PACK))
         with nc.allow_non_contiguous_dma(reason="one offset to a partition"):
-            nc.sync.dma_start(bvec_sb[:], bvec.rearrange("(b p) -> p b", p=P))
+            nc.gpsimd.dma_start(bvec_sb[:], bvec.rearrange("(b p) -> p b", p=P))
+        neg_mu = keep.tile([P, PACK], F32, name="neg_mu")
+        nc.gpsimd.tensor_scalar(neg_mu[:], mu_sb[:], -1.0, 0.0, ALU.mult, ALU.add)
 
         w4_c = keep.tile([P, PASSES, PACK, P], U16, name="w4_c", align_bytes=64)
         w4_s = keep.tile([P, PASSES, PACK, P], U8, name="w4_s", align_bytes=64)
         nc.vector.tensor_copy(w4_c[:], w4_raw[:].bitcast(U16).rearrange("p a (q t) -> p a t q", t=PACK))
-        nc.vector.tensor_copy(w4_s[:], w4s_raw[:].rearrange("p a (q t) -> p a t q", t=PACK))
 
         gsc = keep.tile([P, S], U8, name="gsc", align_bytes=64)
         nc.vector.tensor_copy(gsc[:], tsc[:].indirect(idx[:]))
         for a in range(1, PASSES):
-            nc.gpsimd.dma_start(moved[a - 1][0:112, :].bitcast(I32), gsc[4 * a : 4 * a + 112, :].bitcast(I32))
+            nc.sync.dma_start(moved[a - 1][0:112, :].bitcast(I32), gsc[4 * a : 4 * a + 112, :].bitcast(I32))
         planes = [gsc] + moved
+        nc.vector.tensor_copy(w4_s[:], w4s_raw[:].rearrange("p a (q t) -> p a t q", t=PACK))
+
         w1_c, w1_s = {}, {}
 
         def quantise_w1(a, t0, n, copy):
-            grouped = keep.tile([P, n, P, PACK], BF16, name=f"w1_b{a}_{t0}", align_bytes=64)
+            grouped = keep.tile([P, n, P, PACK], BF16, name=f"w1_b{a}_{t0}", tag=f"rounded{a + t0 // 2}", align_bytes=64)
             src = w1_raw[a][:].rearrange("p j (q t) -> p q j t", t=PACK)[:, :, :, t0 : t0 + n]
             copy(grouped[:].rearrange("p t q j -> p q j t"), src)
             codes = keep.tile([P, n, P], U32, name=f"w1_c{a}_{t0}", align_bytes=64)
@@ -119,16 +125,29 @@ def tile_list_calciner_batch_likeness_kernel(
                 w1_c[a, t0 + t] = codes[:, t, :]
                 w1_s[a, t0 + t] = scales[:, t, :]
 
-        for a in range(PASSES - 1):
-            quantise_w1(a, 0, PACK, nc.scalar.copy)
+        quantise_w1(0, 0, PACK, nc.scalar.copy)
+        load_w1(2)
+        load_wgs(0)
+        quantise_w1(1, 0, PACK, nc.scalar.copy)
+        load_page(0)
+        load_wgs(1)
         gw = {}
         for a in range(PASSES):
             for hf in range(HALVES):
                 gw[a, hf] = keep.tile([P, HALF], U32, name=f"gw{a}_{hf}", align_bytes=64)
                 nc.vector.tensor_copy(gw[a, hf][:], tw[a][:].bitcast(U32).indirect(idx[:, 32 * hf : 32 * hf + 32]))
-        quantise_w1(PASSES - 1, 0, 2, nc.vector.tensor_copy)
+        load_page(1)
+        quantise_w1(2, 0, 2, nc.vector.tensor_copy)
 
-        size, rest, cos_b, abs_a, picked = {}, {}, {}, {}, {}
+        tiles, picked = {}, {}
+
+        def row_tile(name, t, dtype=F32):
+            if (name, t) not in tiles:
+                tiles[name, t] = work.tile([P, S], dtype, name=name, bufs=2)
+            return tiles[name, t]
+
+        def columns(hf0, hf1):
+            return slice(HALF * hf0, HALF * hf1)
 
         def product(acc, codes, scales, hf):
             for a in range(PASSES):
@@ -137,109 +156,111 @@ def tile_list_calciner_batch_likeness_kernel(
                     lhsT=codes[a],
                     lhsT_scale=scales[a],
                     rhs=gw[a, hf][:].bitcast(E4M3X4),
-                    rhs_scale=planes[a][:, HALF * hf : HALF * (hf + 1)],
+                    rhs_scale=planes[a][:, columns(hf, hf + 1)],
                     start=(a == 0),
                     stop=(a == PASSES - 1),
                 )
 
-        def reduce_angles(t, hf):
-            acc = psum.tile([P, HALF], F32, name="acc_b", tag="acc_b")
-            product(
-                acc,
-                [w4_c[:, a, t, :].bitcast(E2M1X4) for a in range(PASSES)],
-                [w4_s[:, a, t, :] for a in range(PASSES)],
-                hf,
-            )
-            size[t, hf] = work.tile([P, HALF], F32, name="size", bufs=4)
-            nc.scalar.activation(size[t, hf][:], acc[:], ACT.Abs)
-            turns = work.tile([P, HALF], U32, name="turns")
-            nc.scalar.activation(turns[:], acc[:], ACT.Abs, scale=1.0 / TWO_PI)
-            rest[t, hf] = work.tile([P, HALF], F32, name="rest")
+        def reduce_angles(t, hf0, hf1):
+            size, turns, rest = row_tile("size", t), row_tile("turns", t, U32), row_tile("rest", t)
+            for hf in range(hf0, hf1):
+                acc = psum.tile([P, HALF], F32, name="acc_b", tag="acc_b")
+                product(
+                    acc,
+                    [w4_c[:, a, t, :].bitcast(E2M1X4) for a in range(PASSES)],
+                    [w4_s[:, a, t, :] for a in range(PASSES)],
+                    hf,
+                )
+                nc.scalar.activation(size[:, columns(hf, hf + 1)], acc[:], ACT.Abs)
+                nc.scalar.activation(turns[:, columns(hf, hf + 1)], acc[:], ACT.Abs, scale=1.0 / TWO_PI)
+            cols = columns(hf0, hf1)
             nc.vector.scalar_tensor_tensor(
-                rest[t, hf][:], turns[:].bitcast(I32), -TWO_PI, size[t, hf][:], ALU.mult, ALU.add
+                rest[:, cols], turns[:, cols].bitcast(I32), -TWO_PI, size[:, cols], ALU.mult, ALU.add
             )
 
-        def cosine(t, hf):
-            folded = work.tile([P, HALF], F32, name="folded", bufs=2)
-            nc.scalar.activation(folded[:], rest[t, hf][:], ACT.Abs)
-            cos_b[t, hf] = work.tile([P, HALF], F32, name="cos_b")
-            nc.scalar.activation(cos_b[t, hf][:], folded[:], ACT.Sin, bias=math.pi / 2, scale=-1.0)
+        def cosine(t, hf0, hf1):
+            cols = columns(hf0, hf1)
+            folded = row_tile("folded", t)
+            nc.scalar.activation(folded[:, cols], row_tile("rest", t)[:, cols], ACT.Abs)
+            nc.scalar.activation(row_tile("cos_b", t)[:, cols], folded[:, cols], ACT.Sin, bias=math.pi / 2, scale=-1.0)
 
-        def magnitudes(t, hf):
-            acc = psum.tile([P, HALF], F32, name="acc_a", tag="acc_a")
-            product(
-                acc,
-                [w1_c[a, t].bitcast(E4M3X4) for a in range(PASSES)],
-                [w1_s[a, t] for a in range(PASSES)],
-                hf,
-            )
-            abs_a[t, hf] = work.tile([P, HALF], F32, name="abs_a")
-            nc.scalar.activation(abs_a[t, hf][:], acc[:], ACT.Abs)
+        def magnitudes(t, hf0, hf1):
+            for hf in range(hf0, hf1):
+                acc = psum.tile([P, HALF], F32, name="acc_a", tag="acc_a")
+                product(
+                    acc,
+                    [w1_c[a, t].bitcast(E4M3X4) for a in range(PASSES)],
+                    [w1_s[a, t] for a in range(PASSES)],
+                    hf,
+                )
+                nc.scalar.activation(row_tile("abs_a", t)[:, columns(hf, hf + 1)], acc[:], ACT.Abs)
 
-        def refresh(t, hf):
-            if hf == 1 and t + 1 < PACK:
-                h = size[t + 1, 1]
-            else:
-                h = work.tile([P, HALF], F32, name="h", bufs=2)
-            nc.vector.tensor_tensor(h[:], abs_a[t, hf][:], cos_b[t, hf][:], ALU.mult)
+        def refresh(t, hf0, hf1):
+            cols = columns(hf0, hf1)
+            h = row_tile("h", t)
+            nc.vector.tensor_tensor(h[:, cols], row_tile("abs_a", t)[:, cols], row_tile("cos_b", t)[:, cols], ALU.mult)
             nc.vector.tensor_tensor(
-                page[t][:].indirect(idx2[:, 32 * hf : 32 * hf + 32]),
-                h[:],
-                wg[t][:, HALF * hf : HALF * (hf + 1)],
-                ALU.mult,
+                page[t][:].indirect(idx2[:, 32 * hf0 : 32 * hf1]), h[:, cols], wg[t][:, cols], ALU.mult
             )
 
-        neg_mu = keep.tile([P, PACK], F32, name="neg_mu")
-        nc.vector.tensor_scalar(neg_mu[:], mu_sb[:], -1.0, None, ALU.mult)
         x1_b = keep.tile([P, M, PACK], BF16, name="x1_b", align_bytes=64)
         x2_b = keep.tile([P, M, PACK], BF16, name="x2_b", align_bytes=64)
 
+        def pieces(t):
+            return [slice(0, M)] if t + 1 < PACK else [slice(0, M // 2), slice(M // 2, M)]
+
         def pick(t):
-            for name, lst in (("ref", idx4), ("new", idx3)):
-                picked[name, t] = work.tile([P, M], F32, name="picked", bufs=6)
-                nc.vector.tensor_copy(picked[name, t][:], page[t][:].indirect(lst[:]))
+            picked["ref", t] = work.tile([P, M], F32, name="picked", bufs=6)
+            for cols in pieces(t):
+                nc.vector.tensor_copy(
+                    picked["ref", t][:, cols], page[t][:].indirect(idx4[:, cols.start // 16 : cols.stop // 16])
+                )
+            picked["new", t] = work.tile([P, M], F32, name="picked", bufs=6)
+            nc.vector.tensor_copy(picked["new", t][:], page[t][:].indirect(idx3[:]))
 
         def reference_rows(t):
             size2 = work.tile([P, M], F32, name="size2", bufs=2)
-            nc.scalar.activation(size2[:], picked["ref", t][:], ACT.Abs)
-            nc.scalar.activation(x2_b[:, :, t], size2[:], ACT.Copy, scale=gain_sb[:, t : t + 1])
+            for cols in pieces(t):
+                nc.scalar.activation(size2[:, cols], picked["ref", t][:, cols], ACT.Abs)
+                nc.scalar.activation(x2_b[:, cols, t], size2[:, cols], ACT.Copy, scale=gain_sb[:, t : t + 1])
 
         def new_rows(t):
             if t < 2:
                 nc.scalar.activation(x1_b[:, :, t], picked["new", t][:], ACT.Identity, bias=neg_mu[:, t : t + 1])
             else:
-                nc.vector.tensor_scalar(x1_b[:, :, t], picked["new", t][:], mu_sb[:, t : t + 1], None, ALU.subtract)
+                nc.vector.tensor_scalar(x1_b[:, :, t], picked["new", t][:], neg_mu[:, t : t + 1], None, ALU.add)
 
-        for hf in range(HALVES):
-            reduce_angles(0, hf)
-        for hf in range(HALVES):
-            cosine(0, hf)
-            magnitudes(0, hf)
-            if hf == 0:
-                refresh(0, 0)
-        for t in range(PACK):
-            more = t + 1 < PACK
-            if more:
-                for hf in range(HALVES):
-                    reduce_angles(t + 1, hf)
-            if t == 0:
-                quantise_w1(PASSES - 1, 2, 2, nc.scalar.copy)
+        reduce_angles(0, 0, 1)
+        reduce_angles(0, 1, 2)
+        cosine(0, 0, 1)
+        magnitudes(0, 0, 1)
+        refresh(0, 0, 1)
+        reduce_angles(1, 0, 2)
+        cosine(0, 1, 2)
+        magnitudes(0, 1, 2)
+        refresh(0, 1, 2)
+        load_page(3)
+        pick(0)
+        for t in range(1, PACK):
+            if t + 1 < PACK:
+                reduce_angles(t + 1, 0, 2)
+            cosine(t, 0, 2)
+            magnitudes(t, 0, 2)
+            if t == 1:
+                quantise_w1(2, 2, 2, nc.scalar.copy)
+                load_page(2)
+                load_wgs(2)
             else:
-                reference_rows(t - 1)
-            refresh(t, 1)
+                reference_rows(t - 2)
+                new_rows(t - 2)
+            refresh(t, 0, 2)
+            if t == 1:
+                load_wgs(3)
             pick(t)
-            if more:
-                for hf in range(HALVES):
-                    cosine(t + 1, hf)
-                for hf in range(HALVES):
-                    magnitudes(t + 1, hf)
-            if t in (1, 2):
-                new_rows(t - 1)
             if t >= 2:
                 new_rows(t)
-            if more:
-                refresh(t + 1, 0)
-        reference_rows(PACK - 1)
+        reference_rows(2)
+        reference_rows(3)
 
         x1_c = keep.tile([P, M], U32, name="x1_c", align_bytes=64)
         x1_s = keep.tile([P, M], U8, name="x1_s", align_bytes=64)

@@ -33,7 +33,7 @@ def tile_list_calciner_batch_likeness_kernel(
         lists = ctx.enter_context(tc.tile_pool(name="lists", bufs=1))
         keep = ctx.enter_context(tc.tile_pool(name="keep", bufs=1))
         work = ctx.enter_context(tc.tile_pool(name="work", bufs=3))
-        psum = ctx.enter_context(tc.psum_pool(name="psum", bufs=4))
+        psum = ctx.enter_context(tc.psum_pool(name="psum", bufs=1))
 
         idx = lists.tile([P, S // 16], U16, name="idx")
         idx2 = lists.tile([P, S // 16], U16, name="idx2")
@@ -53,40 +53,41 @@ def tile_list_calciner_batch_likeness_kernel(
         page_rows = page0.rearrange("(p t) c -> t p c", t=PACK)
 
         def load_w1(a):
-            w1_raw[a] = keep.tile([P, PACK, H], F32, name=f"w1_raw{a}", tag=f"w1_stage{a % 2}", align_bytes=64)
+            w1_raw[a] = keep.tile([P, PACK, H], F32, name=f"w1_raw{a}", tag=f"w1_stage{a}", align_bytes=64)
             nc.sync.dma_start(w1_raw[a][:], w1[512 * a : 512 * (a + 1), :].rearrange("(p j) c -> p j c", j=PACK))
 
         def load_page(t):
             page[t] = keep.tile(
-                [P, T2], F32, name=f"page{t}", tag=("w1_stage1", "table2", "w1_stage0", "rounded0")[t], align_bytes=64
+                [P, T2], F32, name=f"page{t}", tag=("table0", "table2", "w1_stage2", "table1")[t], align_bytes=64
             )
             nc.sync.dma_start(page[t][:], page_rows[t])
 
         def load_wgs(t):
-            wg[t] = keep.tile([P, S], F32, name=f"wg{t}", tag=f"rounded{(0, 1, 3, 1)[t]}", align_bytes=64)
-            for q in range(4):
+            wg[t] = keep.tile([P, S], F32, name=f"wg{t}", tag=f"rounded{(4, 1, 3, 0)[t]}", align_bytes=64)
+            for q in (0, 2, 1, 3):
                 nc.sync.dma_start(wg[t][32 * q : 32 * q + 32, :], wgs_rows[t])
 
-        w4_raw = keep.tile([P, PASSES, 2 * H], U8, name="w4_raw", align_bytes=64)
-        nc.sync.dma_start(w4_raw[:].bitcast(I32), w4_words.rearrange("a p n -> p a n").bitcast(I32))
-        nc.sync.dma_start(idx[:], offs)
-        nc.sync.dma_start(idx2[:], offs2)
-        nc.sync.dma_start(idx4[:], offs4)
-        nc.sync.dma_start(idx3[:], offs3)
-        for a in range(PASSES - 1):
-            load_w1(a)
-        for a in range(PASSES):
+        def load_table(a):
             tw[a] = keep.tile([P, T], I32, name=f"tw{a}", tag=f"table{a}", align_bytes=64)
             nc.sync.dma_start(tw[a][:], tab_words[a].rearrange("p t i -> p (t i)").bitcast(I32))
+
+        w4_raw = keep.tile([P, PASSES, 2 * H], U8, name="w4_raw", align_bytes=64)
+        nc.sync.dma_start(idx[:], offs)
+        nc.sync.dma_start(w4_raw[:].bitcast(I32), w4_words.rearrange("a p n -> p a n").bitcast(I32))
+        load_table(0)
         for q in range(4):
-            nc.scalar.dma_start(
+            nc.sync.dma_start(
                 tsc[32 * q : 32 * q + 4 * PASSES, :].bitcast(I32), tab_scales[:, 4 * q : 4 * q + 4, :].bitcast(I32)
             )
+        load_w1(0)
         for q in range(4):
-            nc.scalar.dma_start(
+            nc.sync.dma_start(
                 w4s_raw[32 * q : 32 * q + 4, :, :].bitcast(I32),
                 w4_scales[:, 4 * q : 4 * q + 4, :].rearrange("a r c -> r a c").bitcast(I32),
             )
+        load_table(1)
+        load_w1(1)
+        load_table(2)
         mu_sb = keep.tile([P, PACK], F32, name="mu_sb")
         gain_sb = keep.tile([P, PACK], F32, name="gain_sb")
         bvec_sb = keep.tile([P, M // P], F32, name="bvec_sb")
@@ -106,14 +107,18 @@ def tile_list_calciner_batch_likeness_kernel(
         for a in range(1, PASSES):
             nc.sync.dma_start(moved[a - 1][0:112, :].bitcast(I32), gsc[4 * a : 4 * a + 112, :].bitcast(I32))
         planes = [gsc] + moved
+        packed = [gsc[4 * a :, :] for a in range(PASSES)]
+        load_w1(2)
+        nc.sync.dma_start(idx2[:], offs2)
+        load_wgs(0)
         nc.vector.tensor_copy(w4_s[:], w4s_raw[:].rearrange("p a (q t) -> p a t q", t=PACK))
 
         w1_c, w1_s = {}, {}
 
         def quantise_w1(a, t0, n, copy):
             grouped = keep.tile([P, n, P, PACK], BF16, name=f"w1_b{a}_{t0}", tag=f"rounded{a + t0 // 2}", align_bytes=64)
-            src = w1_raw[a][:].rearrange("p j (q t) -> p q j t", t=PACK)[:, :, :, t0 : t0 + n]
-            copy(grouped[:].rearrange("p t q j -> p q j t"), src)
+            src = w1_raw[a][:].rearrange("p j (q t) -> p q t j", t=PACK)[:, :, t0 : t0 + n, :]
+            copy(grouped[:].rearrange("p t q j -> p q t j"), src)
             codes = keep.tile([P, n, P], U32, name=f"w1_c{a}_{t0}", align_bytes=64)
             scales = keep.tile([P, n, P], U8, name=f"w1_s{a}_{t0}", align_bytes=64)
             nc.vector.quantize_mx(
@@ -125,19 +130,19 @@ def tile_list_calciner_batch_likeness_kernel(
                 w1_c[a, t0 + t] = codes[:, t, :]
                 w1_s[a, t0 + t] = scales[:, t, :]
 
-        quantise_w1(0, 0, PACK, nc.scalar.copy)
-        load_w1(2)
-        load_wgs(0)
-        quantise_w1(1, 0, PACK, nc.scalar.copy)
-        load_page(0)
-        load_wgs(1)
         gw = {}
         for a in range(PASSES):
             for hf in range(HALVES):
                 gw[a, hf] = keep.tile([P, HALF], U32, name=f"gw{a}_{hf}", align_bytes=64)
                 nc.vector.tensor_copy(gw[a, hf][:], tw[a][:].bitcast(U32).indirect(idx[:, 32 * hf : 32 * hf + 32]))
-        load_page(1)
+        load_page(0)
+        nc.sync.dma_start(idx4[:], offs4)
+        nc.sync.dma_start(idx3[:], offs3)
+        quantise_w1(0, 0, PACK, nc.scalar.copy)
+        quantise_w1(1, 0, PACK, nc.scalar.copy)
         quantise_w1(2, 0, 2, nc.vector.tensor_copy)
+        load_wgs(1)
+        load_page(1)
 
         tiles, picked = {}, {}
 
@@ -149,56 +154,62 @@ def tile_list_calciner_batch_likeness_kernel(
         def columns(hf0, hf1):
             return slice(HALF * hf0, HALF * hf1)
 
-        def product(acc, codes, scales, hf):
+        def product(acc, codes, scales, table_scales, hf):
             for a in range(PASSES):
                 nc.tensor.matmul_mx(
                     acc[:],
                     lhsT=codes[a],
                     lhsT_scale=scales[a],
                     rhs=gw[a, hf][:].bitcast(E4M3X4),
-                    rhs_scale=planes[a][:, columns(hf, hf + 1)],
+                    rhs_scale=table_scales[a][:, columns(hf, hf + 1)],
                     start=(a == 0),
                     stop=(a == PASSES - 1),
                 )
 
-        def reduce_angles(t, hf0, hf1):
-            size, turns, rest = row_tile("size", t), row_tile("turns", t, U32), row_tile("rest", t)
+        def angles(t, hf0, hf1):
+            size, turns = row_tile("size", t), row_tile("turns", t, U32)
             for hf in range(hf0, hf1):
-                acc = psum.tile([P, HALF], F32, name="acc_b", tag="acc_b")
+                acc = psum.tile([P, HALF], F32, name="acc_b", tag=f"bank{min(t, 1)}_{hf}")
                 product(
                     acc,
                     [w4_c[:, a, t, :].bitcast(E2M1X4) for a in range(PASSES)],
                     [w4_s[:, a, t, :] for a in range(PASSES)],
+                    planes,
                     hf,
                 )
                 nc.scalar.activation(size[:, columns(hf, hf + 1)], acc[:], ACT.Abs)
                 nc.scalar.activation(turns[:, columns(hf, hf + 1)], acc[:], ACT.Abs, scale=1.0 / TWO_PI)
+
+        def reduce_angles(t, hf0, hf1, rest):
             cols = columns(hf0, hf1)
-            nc.vector.scalar_tensor_tensor(
-                rest[:, cols], turns[:, cols].bitcast(I32), -TWO_PI, size[:, cols], ALU.mult, ALU.add
-            )
+            tiles["rest", t] = rest
+            turns = row_tile("turns", t, U32)[:, cols].bitcast(I32)
+            nc.vector.scalar_tensor_tensor(rest[:, cols], turns, -TWO_PI, row_tile("size", t)[:, cols], ALU.mult, ALU.add)
 
         def cosine(t, hf0, hf1):
             cols = columns(hf0, hf1)
-            folded = row_tile("folded", t)
-            nc.scalar.activation(folded[:, cols], row_tile("rest", t)[:, cols], ACT.Abs)
-            nc.scalar.activation(row_tile("cos_b", t)[:, cols], folded[:, cols], ACT.Sin, bias=math.pi / 2, scale=-1.0)
+            folded = work.tile([P, HALF * (hf1 - hf0)], F32, name="folded", bufs=1)
+            nc.scalar.activation(folded[:], row_tile("rest", t)[:, cols], ACT.Abs)
+            nc.scalar.activation(row_tile("cos_b", t)[:, cols], folded[:], ACT.Sin, bias=math.pi / 2, scale=-1.0)
 
         def magnitudes(t, hf0, hf1):
             for hf in range(hf0, hf1):
-                acc = psum.tile([P, HALF], F32, name="acc_a", tag="acc_a")
+                acc = psum.tile([P, HALF], F32, name="acc_a", tag=f"bank1_{hf}")
                 product(
                     acc,
                     [w1_c[a, t].bitcast(E4M3X4) for a in range(PASSES)],
                     [w1_s[a, t] for a in range(PASSES)],
+                    packed,
                     hf,
                 )
                 nc.scalar.activation(row_tile("abs_a", t)[:, columns(hf, hf + 1)], acc[:], ACT.Abs)
 
-        def refresh(t, hf0, hf1):
+        def features(t, hf0, hf1, h):
             cols = columns(hf0, hf1)
-            h = row_tile("h", t)
             nc.vector.tensor_tensor(h[:, cols], row_tile("abs_a", t)[:, cols], row_tile("cos_b", t)[:, cols], ALU.mult)
+
+        def refresh(t, hf0, hf1, h):
+            cols = columns(hf0, hf1)
             nc.vector.tensor_tensor(
                 page[t][:].indirect(idx2[:, 32 * hf0 : 32 * hf1]), h[:, cols], wg[t][:, cols], ALU.mult
             )
@@ -216,7 +227,10 @@ def tile_list_calciner_batch_likeness_kernel(
                     picked["ref", t][:, cols], page[t][:].indirect(idx4[:, cols.start // 16 : cols.stop // 16])
                 )
             picked["new", t] = work.tile([P, M], F32, name="picked", bufs=6)
-            nc.vector.tensor_copy(picked["new", t][:], page[t][:].indirect(idx3[:]))
+            for cols in pieces(t):
+                nc.vector.tensor_copy(
+                    picked["new", t][:, cols], page[t][:].indirect(idx3[:, cols.start // 16 : cols.stop // 16])
+                )
 
         def reference_rows(t):
             size2 = work.tile([P, M], F32, name="size2", bufs=2)
@@ -228,65 +242,83 @@ def tile_list_calciner_batch_likeness_kernel(
             if t < 2:
                 nc.scalar.activation(x1_b[:, :, t], picked["new", t][:], ACT.Identity, bias=neg_mu[:, t : t + 1])
             else:
-                nc.vector.tensor_scalar(x1_b[:, :, t], picked["new", t][:], neg_mu[:, t : t + 1], None, ALU.add)
+                for cols in pieces(t):
+                    nc.vector.tensor_scalar(
+                        x1_b[:, cols, t], picked["new", t][:, cols], neg_mu[:, t : t + 1], None, ALU.add
+                    )
 
-        reduce_angles(0, 0, 1)
-        reduce_angles(0, 1, 2)
+        rest0 = keep.tile([P, S], F32, name="rest0", tag="rounded2", align_bytes=64)
+        h = keep.tile([P, S], F32, name="h0", tag="rounded3", align_bytes=64)
+        for hf in range(HALVES):
+            angles(0, hf, hf + 1)
+            reduce_angles(0, hf, hf + 1, rest0)
         cosine(0, 0, 1)
         magnitudes(0, 0, 1)
-        refresh(0, 0, 1)
-        reduce_angles(1, 0, 2)
+        features(0, 0, 1, h)
+        refresh(0, 0, 1, h)
         cosine(0, 1, 2)
         magnitudes(0, 1, 2)
-        refresh(0, 1, 2)
-        load_page(3)
-        pick(0)
-        for t in range(1, PACK):
-            if t + 1 < PACK:
-                reduce_angles(t + 1, 0, 2)
-            cosine(t, 0, 2)
-            magnitudes(t, 0, 2)
-            if t == 1:
-                quantise_w1(2, 2, 2, nc.scalar.copy)
-                load_page(2)
-                load_wgs(2)
-            else:
-                reference_rows(t - 2)
-                new_rows(t - 2)
-            refresh(t, 0, 2)
-            if t == 1:
-                load_wgs(3)
+        angles(1, 0, 2)
+        reduce_angles(1, 0, 2, h)
+        h = row_tile("size", 1)
+        features(0, 1, 2, h)
+        refresh(0, 1, 2, h)
+        for t in range(PACK):
             pick(t)
             if t >= 2:
                 new_rows(t)
-        reference_rows(2)
-        reference_rows(3)
+            if t + 1 < PACK:
+                cosine(t + 1, 0, 2)
+                magnitudes(t + 1, 0, 2)
+                features(t + 1, 0, 2, wg[t])
+            if t + 2 < PACK:
+                angles(t + 2, 0, 2)
+                reduce_angles(t + 2, 0, 2, h)
+            if t == 0:
+                quantise_w1(2, 2, 2, nc.scalar.copy)
+                load_page(2)
+                load_wgs(2)
+                load_page(3)
+                load_wgs(3)
+            else:
+                reference_rows(t - 1)
+                if t <= 2:
+                    new_rows(t - 1)
+            if t + 1 < PACK:
+                h = wg[t]
+                refresh(t + 1, 0, 2, h)
+        reference_rows(PACK - 1)
 
         x1_c = keep.tile([P, M], U32, name="x1_c", align_bytes=64)
         x1_s = keep.tile([P, M], U8, name="x1_s", align_bytes=64)
         x2_c = keep.tile([P, M], U32, name="x2_c", align_bytes=64)
         x2_s = keep.tile([P, M], U8, name="x2_s", align_bytes=64)
-        nc.vector.quantize_mx(x2_c[:].bitcast(E4M3X4), x2_s[:], x2_b[:].rearrange("p m t -> p (m t)"))
-        for b in range(M // P):
-            rows = slice(P * b, P * (b + 1))
+        def quantise(codes, scales, rounded, cols):
             nc.vector.quantize_mx(
-                x1_c[:, rows].bitcast(E4M3X4), x1_s[:, rows], x1_b[:, rows, :].rearrange("p m t -> p (m t)")
+                codes[:, cols].bitcast(E4M3X4), scales[:, cols], rounded[:, cols, :].rearrange("p m t -> p (m t)")
             )
-        for b in range(M // P):
-            rows = slice(P * b, P * (b + 1))
-            acc = psum.tile([P, M], F32, name="acc_e", tag=("acc_a", "acc_b")[b % 2])
-            nc.tensor.matmul_mx(
-                acc[:],
-                lhsT=x1_c[:, rows].bitcast(E4M3X4),
-                lhsT_scale=x1_s[:, rows],
-                rhs=x2_c[:].bitcast(E4M3X4),
-                rhs_scale=x2_s[:],
-                start=True,
-                stop=True,
-            )
-            res = work.tile([P, M], F32, name="res", tag="picked", bufs=6)
-            if b % 2 == 0:
-                nc.scalar.activation(res[:], acc[:], ACT.Identity, bias=bvec_sb[:, b : b + 1])
-            else:
-                nc.vector.tensor_scalar(res[:], acc[:], bvec_sb[:, b : b + 1], None, ALU.add)
-            nc.sync.dma_start(out[rows, :], res[:])
+
+        halves = pieces(PACK - 1)
+        for cols in halves:
+            quantise(x2_c, x2_s, x2_b, cols)
+            quantise(x1_c, x1_s, x1_b, cols)
+        for pair, hf in ((0, 0), (0, 1), (1, 0), (1, 1)):
+            cols = halves[hf]
+            for b in (2 * pair, 2 * pair + 1):
+                rows = slice(P * b, P * (b + 1))
+                acc = psum.tile([P, M // 2], F32, name="acc_e", tag=(f"result{b}", f"bank{b // 2}_{b % 2}")[hf])
+                nc.tensor.matmul_mx(
+                    acc[:],
+                    lhsT=x1_c[:, rows].bitcast(E4M3X4),
+                    lhsT_scale=x1_s[:, rows],
+                    rhs=x2_c[:, cols].bitcast(E4M3X4),
+                    rhs_scale=x2_s[:, cols],
+                    start=True,
+                    stop=True,
+                )
+                res = work.tile([P, M // 2], F32, name="res", bufs=8)
+                if pair == 0 or b % 2 == 0:
+                    nc.scalar.activation(res[:], acc[:], ACT.Identity, bias=bvec_sb[:, b : b + 1])
+                else:
+                    nc.vector.tensor_scalar(res[:], acc[:], bvec_sb[:, b : b + 1], None, ALU.add)
+                nc.sync.dma_start(out[rows, cols], res[:])

@@ -48,6 +48,9 @@ def tile_list_calciner_batch_likeness_kernel(
         for plane in moved:
             nc.vector.memset(plane[:].bitcast(I32), 0)
 
+        warm = keep.tile([P, 2], F32, name="warm")
+        nc.gpsimd.memset(warm[:, 0:1], 0.0)
+        nc.scalar.activation(warm[:, 1:2], warm[:, 0:1], ACT.Sin)
         w1_raw, tw, wg, page = {}, {}, {}, {}
         wgs_rows = wgs.rearrange("(q t) s -> t q s", t=PACK)
         page_rows = page0.rearrange("(p t) c -> t p c", t=PACK)
@@ -91,12 +94,6 @@ def tile_list_calciner_batch_likeness_kernel(
         mu_sb = keep.tile([P, PACK], F32, name="mu_sb")
         gain_sb = keep.tile([P, PACK], F32, name="gain_sb")
         bvec_sb = keep.tile([P, M // P], F32, name="bvec_sb")
-        nc.gpsimd.dma_start(mu_sb[:], mu.rearrange("(p t) -> p t", t=PACK))
-        nc.gpsimd.dma_start(gain_sb[:], gain.rearrange("(p t) -> p t", t=PACK))
-        with nc.allow_non_contiguous_dma(reason="one offset to a partition"):
-            nc.gpsimd.dma_start(bvec_sb[:], bvec.rearrange("(b p) -> p b", p=P))
-        neg_mu = keep.tile([P, PACK], F32, name="neg_mu")
-        nc.gpsimd.tensor_scalar(neg_mu[:], mu_sb[:], -1.0, 0.0, ALU.mult, ALU.add)
 
         w4_c = keep.tile([P, PASSES, PACK, P], U16, name="w4_c", align_bytes=64)
         w4_s = keep.tile([P, PASSES, PACK, P], U8, name="w4_s", align_bytes=64)
@@ -138,6 +135,10 @@ def tile_list_calciner_batch_likeness_kernel(
         load_page(0)
         nc.sync.dma_start(idx4[:], offs4)
         nc.sync.dma_start(idx3[:], offs3)
+        nc.sync.dma_start(mu_sb[:], mu.rearrange("(p t) -> p t", t=PACK))
+        nc.sync.dma_start(gain_sb[:], gain.rearrange("(p t) -> p t", t=PACK))
+        neg_mu = keep.tile([P, PACK], F32, name="neg_mu")
+        nc.scalar.activation(neg_mu[:], mu_sb[:], ACT.Copy, scale=-1.0)
         quantise_w1(0, 0, PACK, nc.scalar.copy)
         quantise_w1(1, 0, PACK, nc.scalar.copy)
         quantise_w1(2, 0, 2, nc.vector.tensor_copy)
@@ -206,7 +207,8 @@ def tile_list_calciner_batch_likeness_kernel(
 
         def features(t, hf0, hf1, h):
             cols = columns(hf0, hf1)
-            nc.vector.tensor_tensor(h[:, cols], row_tile("abs_a", t)[:, cols], row_tile("cos_b", t)[:, cols], ALU.mult)
+            engine = nc.vector if t == 0 else nc.gpsimd
+            engine.tensor_tensor(h[:, cols], row_tile("abs_a", t)[:, cols], row_tile("cos_b", t)[:, cols], ALU.mult)
 
         def refresh(t, hf0, hf1, h):
             cols = columns(hf0, hf1)
@@ -280,6 +282,8 @@ def tile_list_calciner_batch_likeness_kernel(
                 load_wgs(2)
                 load_page(3)
                 load_wgs(3)
+                with nc.allow_non_contiguous_dma(reason="one offset to a partition"):
+                    nc.sync.dma_start(bvec_sb[:], bvec.rearrange("(b p) -> p b", p=P))
             else:
                 reference_rows(t - 1)
                 if t <= 2:

@@ -19,10 +19,27 @@ ALU = mybir.AluOpType
 
 P = 128
 PACK = 4
-PASSES = K // (P * PACK)
-HALF = 512
-HALVES = S // HALF
+PASS = P * PACK
+PASSES = K // PASS
+QUADRANT = 32
+QUADRANTS = P // QUADRANT
+BLOCKS = 4
+PLANE_ROWS = P - QUADRANT + BLOCKS
+PER_COLUMN = 16
+BANK = 512
+FIRST, SECOND, ALL = slice(0, BANK), slice(BANK, S), slice(0, S)
+BANK_SPANS = (FIRST, SECOND)
+LEFT, RIGHT, BOTH = slice(0, M // 2), slice(M // 2, M), slice(0, M)
+LAST = PACK - 1
 TWO_PI = 2.0 * math.pi
+
+
+def entries(offsets, span):
+    return offsets[:, span.start // PER_COLUMN : span.stop // PER_COLUMN]
+
+
+def banks_of(span):
+    return range(span.start // BANK, span.stop // BANK)
 
 
 def tile_list_calciner_batch_likeness_kernel(
@@ -32,297 +49,287 @@ def tile_list_calciner_batch_likeness_kernel(
     with ExitStack() as ctx:
         lists = ctx.enter_context(tc.tile_pool(name="lists", bufs=1))
         keep = ctx.enter_context(tc.tile_pool(name="keep", bufs=1))
-        work = ctx.enter_context(tc.tile_pool(name="work", bufs=3))
+        work = ctx.enter_context(tc.tile_pool(name="work", bufs=2))
         psum = ctx.enter_context(tc.psum_pool(name="psum", bufs=1))
 
-        idx = lists.tile([P, S // 16], U16, name="idx")
-        idx2 = lists.tile([P, S // 16], U16, name="idx2")
-        idx3 = lists.tile([P, M // 16], U16, name="idx3")
-        idx4 = lists.tile([P, M // 16], U16, name="idx4")
+        def held(shape, dtype, name, tag=None):
+            return keep.tile(shape, dtype, name=name, tag=tag or name, align_bytes=64)
 
-        tsc = keep.tile([P, T], U8, name="tsc", align_bytes=64)
-        w4s_raw = keep.tile([P, PASSES, H], U8, name="w4s_raw", align_bytes=64)
-        moved = [keep.tile([P, S], U8, name=f"moved{a}", align_bytes=64) for a in range(1, PASSES)]
-        nc.vector.memset(tsc[:].bitcast(I32), 0)
-        nc.vector.memset(w4s_raw[:].rearrange("p a c -> p (a c)").bitcast(I32), 0)
-        for plane in moved:
+        idx = lists.tile([P, S // PER_COLUMN], U16, name="idx")
+        idx2 = lists.tile([P, S // PER_COLUMN], U16, name="idx2")
+        idx3 = lists.tile([P, M // PER_COLUMN], U16, name="idx3")
+        idx4 = lists.tile([P, M // PER_COLUMN], U16, name="idx4")
+
+        table_scales = held([P, T], U8, "table_scales")
+        w4_scales_raw = held([P, PASSES, H], U8, "w4_scales_raw")
+        moved_planes = [held([P, S], U8, f"moved_plane{a}") for a in range(1, PASSES)]
+        nc.vector.memset(table_scales[:].bitcast(I32), 0)
+        nc.vector.memset(w4_scales_raw[:].rearrange("p a c -> p (a c)").bitcast(I32), 0)
+        for plane in moved_planes:
             nc.vector.memset(plane[:].bitcast(I32), 0)
 
         warm = keep.tile([P, 2], F32, name="warm")
         nc.gpsimd.memset(warm[:, 0:1], 0.0)
         nc.scalar.activation(warm[:, 1:2], warm[:, 0:1], ACT.Sin)
-        w1_raw, tw, wg, page = {}, {}, {}, {}
+
+        w1_raw, table_words, weights, page = {}, {}, {}, {}
         wgs_rows = wgs.rearrange("(q t) s -> t q s", t=PACK)
         page_rows = page0.rearrange("(p t) c -> t p c", t=PACK)
 
         def load_w1(a):
-            w1_raw[a] = keep.tile([P, PACK, H], F32, name=f"w1_raw{a}", tag=f"w1_stage{a}", align_bytes=64)
-            nc.sync.dma_start(w1_raw[a][:], w1[512 * a : 512 * (a + 1), :].rearrange("(p j) c -> p j c", j=PACK))
-
-        def load_page(t):
-            page[t] = keep.tile(
-                [P, T2], F32, name=f"page{t}", tag=("table0", "table2", "w1_stage2", "table1")[t], align_bytes=64
-            )
-            nc.sync.dma_start(page[t][:], page_rows[t])
-
-        def load_wgs(t):
-            wg[t] = keep.tile([P, S], F32, name=f"wg{t}", tag=f"rounded{(4, 1, 3, 0)[t]}", align_bytes=64)
-            for q in (0, 2, 1, 3):
-                nc.sync.dma_start(wg[t][32 * q : 32 * q + 32, :], wgs_rows[t])
+            w1_raw[a] = held([P, PACK, H], F32, f"w1_raw{a}")
+            nc.sync.dma_start(w1_raw[a][:], w1[PASS * a : PASS * (a + 1), :].rearrange("(p j) c -> p j c", j=PACK))
 
         def load_table(a):
-            tw[a] = keep.tile([P, T], I32, name=f"tw{a}", tag=f"table{a}", align_bytes=64)
-            nc.sync.dma_start(tw[a][:], tab_words[a].rearrange("p t i -> p (t i)").bitcast(I32))
+            table_words[a] = held([P, T], I32, f"table_words{a}")
+            nc.sync.dma_start(table_words[a][:], tab_words[a].rearrange("p t i -> p (t i)").bitcast(I32))
 
-        w4_raw = keep.tile([P, PASSES, 2 * H], U8, name="w4_raw", align_bytes=64)
+        def load_page(t):
+            page[t] = held([P, T2], F32, f"page{t}")
+            nc.sync.dma_start(page[t][:], page_rows[t])
+
+        def load_weights(t, span):
+            if span.start == 0:
+                weights[t] = held([P, S], F32, f"weights{t}")
+            for q in (0, 2, 1, 3):
+                nc.sync.dma_start(weights[t][QUADRANT * q : QUADRANT * (q + 1), span], wgs_rows[t][:, span])
+
+        w4_raw = held([P, PASSES, 2 * H], U8, "w4_raw")
         nc.sync.dma_start(idx[:], offs)
         nc.sync.dma_start(w4_raw[:].bitcast(I32), w4_words.rearrange("a p n -> p a n").bitcast(I32))
         load_table(0)
-        for q in range(4):
+        for q in range(QUADRANTS):
             nc.sync.dma_start(
-                tsc[32 * q : 32 * q + 4 * PASSES, :].bitcast(I32), tab_scales[:, 4 * q : 4 * q + 4, :].bitcast(I32)
+                table_scales[QUADRANT * q : QUADRANT * q + BLOCKS * PASSES, :].bitcast(I32),
+                tab_scales[:, BLOCKS * q : BLOCKS * (q + 1), :].bitcast(I32),
             )
         load_w1(0)
-        for q in range(4):
+        for q in range(QUADRANTS):
             nc.sync.dma_start(
-                w4s_raw[32 * q : 32 * q + 4, :, :].bitcast(I32),
-                w4_scales[:, 4 * q : 4 * q + 4, :].rearrange("a r c -> r a c").bitcast(I32),
+                w4_scales_raw[QUADRANT * q : QUADRANT * q + BLOCKS, :, :].bitcast(I32),
+                w4_scales[:, BLOCKS * q : BLOCKS * (q + 1), :].rearrange("a r c -> r a c").bitcast(I32),
             )
         load_table(1)
         load_w1(1)
         load_table(2)
-        mu_sb = keep.tile([P, PACK], F32, name="mu_sb")
-        gain_sb = keep.tile([P, PACK], F32, name="gain_sb")
-        bvec_sb = keep.tile([P, M // P], F32, name="bvec_sb")
 
-        w4_c = keep.tile([P, PASSES, PACK, P], U16, name="w4_c", align_bytes=64)
-        w4_s = keep.tile([P, PASSES, PACK, P], U8, name="w4_s", align_bytes=64)
-        nc.vector.tensor_copy(w4_c[:], w4_raw[:].bitcast(U16).rearrange("p a (q t) -> p a t q", t=PACK))
+        w4_codes = held([P, PASSES, PACK, P], U16, "w4_codes")
+        w4_planes = held([P, PASSES, PACK, P], U8, "w4_planes")
+        nc.vector.tensor_copy(w4_codes[:], w4_raw[:].bitcast(U16).rearrange("p a (q t) -> p a t q", t=PACK))
 
-        gsc = keep.tile([P, S], U8, name="gsc", align_bytes=64)
-        nc.vector.tensor_copy(gsc[:], tsc[:].indirect(idx[:]))
+        picked_scales = held([P, S], U8, "picked_scales")
+        nc.vector.tensor_copy(picked_scales[:], table_scales[:].indirect(idx[:]))
         for a in range(1, PASSES):
-            nc.sync.dma_start(moved[a - 1][0:112, :].bitcast(I32), gsc[4 * a : 4 * a + 112, :].bitcast(I32))
-        planes = [gsc] + moved
-        packed = [gsc[4 * a :, :] for a in range(PASSES)]
+            nc.sync.dma_start(
+                moved_planes[a - 1][0:PLANE_ROWS, :].bitcast(I32),
+                picked_scales[BLOCKS * a : BLOCKS * a + PLANE_ROWS, :].bitcast(I32),
+            )
+        planes_for_w4 = [picked_scales] + moved_planes
+        planes_for_w1 = [picked_scales[BLOCKS * a :, :] for a in range(PASSES)]
         load_w1(2)
         nc.sync.dma_start(idx2[:], offs2)
-        load_wgs(0)
-        nc.vector.tensor_copy(w4_s[:], w4s_raw[:].rearrange("p a (q t) -> p a t q", t=PACK))
+        load_weights(0, FIRST)
+        nc.vector.tensor_copy(w4_planes[:], w4_scales_raw[:].rearrange("p a (q t) -> p a t q", t=PACK))
 
-        w1_c, w1_s = {}, {}
+        picked_words = {}
+        for a in range(PASSES):
+            for n, span in enumerate(BANK_SPANS):
+                picked_words[a, n] = held([P, BANK], U32, f"picked_words{a}_{n}")
+                nc.vector.tensor_copy(
+                    picked_words[a, n][:], table_words[a][:].bitcast(U32).indirect(entries(idx, span))
+                )
 
-        def quantise_w1(a, t0, n, copy):
-            grouped = keep.tile([P, n, P, PACK], BF16, name=f"w1_b{a}_{t0}", tag=f"rounded{a + t0 // 2}", align_bytes=64)
-            src = w1_raw[a][:].rearrange("p j (q t) -> p q t j", t=PACK)[:, :, t0 : t0 + n, :]
-            copy(grouped[:].rearrange("p t q j -> p q t j"), src)
-            codes = keep.tile([P, n, P], U32, name=f"w1_c{a}_{t0}", align_bytes=64)
-            scales = keep.tile([P, n, P], U8, name=f"w1_s{a}_{t0}", align_bytes=64)
+        mu_rows = keep.tile([P, PACK], F32, name="mu_rows")
+        gain_rows = keep.tile([P, PACK], F32, name="gain_rows")
+        minus_mu = keep.tile([P, PACK], F32, name="minus_mu")
+        bvec_rows = keep.tile([P, M // P], F32, name="bvec_rows")
+        load_page(0)
+        load_weights(0, SECOND)
+        nc.sync.dma_start(idx4[:], offs4)
+        nc.sync.dma_start(idx3[:], offs3)
+        nc.sync.dma_start(mu_rows[:], mu.rearrange("(p t) -> p t", t=PACK))
+        nc.sync.dma_start(gain_rows[:], gain.rearrange("(p t) -> p t", t=PACK))
+        nc.scalar.activation(minus_mu[:], mu_rows[:], ACT.Copy, scale=-1.0)
+
+        w1_codes, w1_planes = {}, {}
+
+        def quantise_w1(a, t0, count, copy, rounded_tag=None, codes_tag=None):
+            rounded = held([P, count, P, PACK], BF16, f"w1_rounded{a}_{t0}", rounded_tag)
+            source = w1_raw[a][:].rearrange("p j (q t) -> p q j t", t=PACK)[:, :, :, t0 : t0 + count]
+            copy(rounded[:].rearrange("p t q j -> p q j t"), source)
+            codes = held([P, count, P], U32, f"w1_codes{a}_{t0}", codes_tag)
+            scales = held([P, count, P], U8, f"w1_planes{a}_{t0}")
             nc.vector.quantize_mx(
                 codes[:].rearrange("p t q -> p (t q)").bitcast(E4M3X4),
                 scales[:].rearrange("p t q -> p (t q)"),
-                grouped[:].rearrange("p t q j -> p (t q j)"),
+                rounded[:].rearrange("p t q j -> p (t q j)"),
             )
-            for t in range(n):
-                w1_c[a, t0 + t] = codes[:, t, :]
-                w1_s[a, t0 + t] = scales[:, t, :]
+            for t in range(count):
+                w1_codes[a, t0 + t] = codes[:, t, :]
+                w1_planes[a, t0 + t] = scales[:, t, :]
 
-        gw = {}
-        for a in range(PASSES):
-            for hf in range(HALVES):
-                gw[a, hf] = keep.tile([P, HALF], U32, name=f"gw{a}_{hf}", align_bytes=64)
-                nc.vector.tensor_copy(gw[a, hf][:], tw[a][:].bitcast(U32).indirect(idx[:, 32 * hf : 32 * hf + 32]))
-        load_page(0)
-        nc.sync.dma_start(idx4[:], offs4)
-        nc.sync.dma_start(idx3[:], offs3)
-        nc.sync.dma_start(mu_sb[:], mu.rearrange("(p t) -> p t", t=PACK))
-        nc.sync.dma_start(gain_sb[:], gain.rearrange("(p t) -> p t", t=PACK))
-        neg_mu = keep.tile([P, PACK], F32, name="neg_mu")
-        nc.scalar.activation(neg_mu[:], mu_sb[:], ACT.Copy, scale=-1.0)
-        quantise_w1(0, 0, PACK, nc.scalar.copy)
-        quantise_w1(1, 0, PACK, nc.scalar.copy)
-        quantise_w1(2, 0, 2, nc.vector.tensor_copy)
-        load_wgs(1)
+        for a in range(PASSES - 1):
+            quantise_w1(a, 0, PACK, nc.scalar.copy, codes_tag=f"table_words{a + 1}")
+        quantise_w1(2, 0, 2, nc.vector.tensor_copy, rounded_tag="late_rounded")
+        load_weights(1, ALL)
         load_page(1)
 
-        tiles, picked = {}, {}
+        rows = {}
 
         def row_tile(name, t, dtype=F32):
-            if (name, t) not in tiles:
-                tiles[name, t] = work.tile([P, S], dtype, name=name, bufs=2)
-            return tiles[name, t]
+            if (name, t) not in rows:
+                rows[name, t] = work.tile([P, S], dtype, name=name)
+            return rows[name, t]
 
-        def columns(hf0, hf1):
-            return slice(HALF * hf0, HALF * hf1)
-
-        def product(acc, codes, scales, table_scales, hf):
+        def product(acc, codes, scales, table_planes, n):
             for a in range(PASSES):
                 nc.tensor.matmul_mx(
                     acc[:],
                     lhsT=codes[a],
                     lhsT_scale=scales[a],
-                    rhs=gw[a, hf][:].bitcast(E4M3X4),
-                    rhs_scale=table_scales[a][:, columns(hf, hf + 1)],
+                    rhs=picked_words[a, n][:].bitcast(E4M3X4),
+                    rhs_scale=table_planes[a][:, BANK_SPANS[n]],
                     start=(a == 0),
                     stop=(a == PASSES - 1),
                 )
 
-        def angles(t, hf0, hf1):
-            size, turns = row_tile("size", t), row_tile("turns", t, U32)
-            for hf in range(hf0, hf1):
-                acc = psum.tile([P, HALF], F32, name="acc_b", tag=f"bank{min(t, 1)}_{hf}")
-                product(
-                    acc,
-                    [w4_c[:, a, t, :].bitcast(E2M1X4) for a in range(PASSES)],
-                    [w4_s[:, a, t, :] for a in range(PASSES)],
-                    planes,
-                    hf,
-                )
-                nc.scalar.activation(size[:, columns(hf, hf + 1)], acc[:], ACT.Abs)
-                nc.scalar.activation(turns[:, columns(hf, hf + 1)], acc[:], ACT.Abs, scale=1.0 / TWO_PI)
+        def angles(t, span):
+            for n in banks_of(span):
+                acc = psum.tile([P, BANK], F32, name="acc_b", tag=f"first_angles{n}" if t == 0 else f"sums{n}")
+                codes = [w4_codes[:, a, t, :].bitcast(E2M1X4) for a in range(PASSES)]
+                product(acc, codes, [w4_planes[:, a, t, :] for a in range(PASSES)], planes_for_w4, n)
+                nc.scalar.activation(row_tile("abs_b", t)[:, BANK_SPANS[n]], acc[:], ACT.Abs)
+                nc.scalar.activation(row_tile("turns", t, U32)[:, BANK_SPANS[n]], acc[:], ACT.Abs, scale=1.0 / TWO_PI)
 
-        def reduce_angles(t, hf0, hf1, rest):
-            cols = columns(hf0, hf1)
-            tiles["rest", t] = rest
-            turns = row_tile("turns", t, U32)[:, cols].bitcast(I32)
-            nc.vector.scalar_tensor_tensor(rest[:, cols], turns, -TWO_PI, row_tile("size", t)[:, cols], ALU.mult, ALU.add)
+        def reduce_angles(t, span, rest):
+            turns = row_tile("turns", t, U32)[:, span].bitcast(I32)
+            nc.vector.scalar_tensor_tensor(rest, turns, -TWO_PI, row_tile("abs_b", t)[:, span], ALU.mult, ALU.add)
 
-        def cosine(t, hf0, hf1):
-            cols = columns(hf0, hf1)
-            folded = work.tile([P, HALF * (hf1 - hf0)], F32, name="folded", bufs=1)
-            nc.scalar.activation(folded[:], row_tile("rest", t)[:, cols], ACT.Abs)
-            nc.scalar.activation(row_tile("cos_b", t)[:, cols], folded[:], ACT.Sin, bias=math.pi / 2, scale=-1.0)
+        def cosine(t, span, rest):
+            folded = work.tile([P, span.stop - span.start], F32, name="folded", bufs=1)
+            nc.scalar.activation(folded[:], rest, ACT.Abs)
+            nc.scalar.activation(row_tile("cos_b", t)[:, span], folded[:], ACT.Sin, bias=math.pi / 2, scale=-1.0)
 
-        def magnitudes(t, hf0, hf1):
-            for hf in range(hf0, hf1):
-                acc = psum.tile([P, HALF], F32, name="acc_a", tag=f"bank1_{hf}")
-                product(
-                    acc,
-                    [w1_c[a, t].bitcast(E4M3X4) for a in range(PASSES)],
-                    [w1_s[a, t] for a in range(PASSES)],
-                    packed,
-                    hf,
-                )
-                nc.scalar.activation(row_tile("abs_a", t)[:, columns(hf, hf + 1)], acc[:], ACT.Abs)
+        def magnitudes(t, span):
+            for n in banks_of(span):
+                acc = psum.tile([P, BANK], F32, name="acc_a", tag=f"sums{n}")
+                codes = [w1_codes[a, t].bitcast(E4M3X4) for a in range(PASSES)]
+                product(acc, codes, [w1_planes[a, t] for a in range(PASSES)], planes_for_w1, n)
+                nc.scalar.activation(row_tile("abs_a", t)[:, BANK_SPANS[n]], acc[:], ACT.Abs)
 
-        def features(t, hf0, hf1, h):
-            cols = columns(hf0, hf1)
-            engine = nc.vector if t == 0 else nc.gpsimd
-            engine.tensor_tensor(h[:, cols], row_tile("abs_a", t)[:, cols], row_tile("cos_b", t)[:, cols], ALU.mult)
+        def features(t, span, h):
+            nc.vector.tensor_tensor(h[:, span], row_tile("abs_a", t)[:, span], row_tile("cos_b", t)[:, span], ALU.mult)
 
-        def refresh(t, hf0, hf1, h):
-            cols = columns(hf0, hf1)
-            nc.vector.tensor_tensor(
-                page[t][:].indirect(idx2[:, 32 * hf0 : 32 * hf1]), h[:, cols], wg[t][:, cols], ALU.mult
-            )
+        def refresh(t, span, h):
+            nc.vector.tensor_tensor(page[t][:].indirect(entries(idx2, span)), h[:, span], weights[t][:, span], ALU.mult)
 
-        x1_b = keep.tile([P, M, PACK], BF16, name="x1_b", align_bytes=64)
-        x2_b = keep.tile([P, M, PACK], BF16, name="x2_b", align_bytes=64)
+        x1_rounded = held([P, M, PACK], BF16, "x1_rounded")
+        x2_rounded = held([P, M, PACK], BF16, "x2_rounded")
+        picked_ref, picked_new = {}, {}
+        picks_alive = 6
 
-        def pieces(t):
-            return [slice(0, M)] if t + 1 < PACK else [slice(0, M // 2), slice(M // 2, M)]
+        def spans_of(t):
+            return (LEFT, RIGHT) if t == LAST else (BOTH,)
 
         def pick(t):
-            picked["ref", t] = work.tile([P, M], F32, name="picked", bufs=6)
-            for cols in pieces(t):
-                nc.vector.tensor_copy(
-                    picked["ref", t][:, cols], page[t][:].indirect(idx4[:, cols.start // 16 : cols.stop // 16])
-                )
-            picked["new", t] = work.tile([P, M], F32, name="picked", bufs=6)
-            for cols in pieces(t):
-                nc.vector.tensor_copy(
-                    picked["new", t][:, cols], page[t][:].indirect(idx3[:, cols.start // 16 : cols.stop // 16])
-                )
+            for picked, offsets in ((picked_ref, idx4), (picked_new, idx3)):
+                picked[t] = work.tile([P, M], F32, name="picked", bufs=picks_alive)
+                for span in spans_of(t):
+                    nc.vector.tensor_copy(picked[t][:, span], page[t][:].indirect(entries(offsets, span)))
 
         def reference_rows(t):
-            size2 = work.tile([P, M], F32, name="size2", bufs=2)
-            for cols in pieces(t):
-                nc.scalar.activation(size2[:, cols], picked["ref", t][:, cols], ACT.Abs)
-                nc.scalar.activation(x2_b[:, cols, t], size2[:, cols], ACT.Copy, scale=gain_sb[:, t : t + 1])
+            abs_ref = work.tile([P, M], F32, name="abs_ref")
+            for span in spans_of(t):
+                nc.scalar.activation(abs_ref[:, span], picked_ref[t][:, span], ACT.Abs)
+                nc.scalar.activation(x2_rounded[:, span, t], abs_ref[:, span], ACT.Copy, scale=gain_rows[:, t : t + 1])
+
+        last_pair = held([P, 2, M], BF16, "last_pair")
 
         def new_rows(t):
-            if t < 2:
-                nc.scalar.activation(x1_b[:, :, t], picked["new", t][:], ACT.Identity, bias=neg_mu[:, t : t + 1])
+            shift = minus_mu[:, t : t + 1]
+            if t < LAST:
+                rounded = x1_rounded[:, :, t] if t < 2 else last_pair[:, 0, :]
+                nc.scalar.activation(rounded, picked_new[t][:], ACT.Identity, bias=shift)
             else:
-                for cols in pieces(t):
-                    nc.vector.tensor_scalar(
-                        x1_b[:, cols, t], picked["new", t][:, cols], neg_mu[:, t : t + 1], None, ALU.add
-                    )
+                for span in spans_of(t):
+                    nc.vector.tensor_scalar(last_pair[:, 1, span], picked_new[t][:, span], shift, None, ALU.add)
+                for span in spans_of(t):
+                    pair_by_column = last_pair[:, :, span].rearrange("p t m -> p m t")
+                    nc.vector.tensor_copy(x1_rounded[:, span, 2:PACK], pair_by_column)
 
-        rest0 = keep.tile([P, S], F32, name="rest0", tag="rounded2", align_bytes=64)
-        h = keep.tile([P, S], F32, name="h0", tag="rounded3", align_bytes=64)
-        for hf in range(HALVES):
-            angles(0, hf, hf + 1)
-            reduce_angles(0, hf, hf + 1, rest0)
-        cosine(0, 0, 1)
-        magnitudes(0, 0, 1)
-        features(0, 0, 1, h)
-        refresh(0, 0, 1, h)
-        cosine(0, 1, 2)
-        magnitudes(0, 1, 2)
-        angles(1, 0, 2)
-        reduce_angles(1, 0, 2, h)
-        h = row_tile("size", 1)
-        features(0, 1, 2, h)
-        refresh(0, 1, 2, h)
+        rest_first = held([P, BANK], F32, "rest_first")
+        rest_second = held([P, BANK], F32, "rest_second", "late_rounded")
+        h = held([P, S], F32, "first_features")
+        angles(0, FIRST)
+        reduce_angles(0, FIRST, rest_first[:])
+        angles(0, SECOND)
+        reduce_angles(0, SECOND, rest_second[:])
+        cosine(0, FIRST, rest_first[:])
+        magnitudes(0, FIRST)
+        features(0, FIRST, h)
+        refresh(0, FIRST, h)
+        cosine(0, SECOND, rest_second[:])
+        magnitudes(0, SECOND)
+        angles(1, ALL)
+        rest = h
+        reduce_angles(1, ALL, rest[:])
+        h = row_tile("abs_b", 1)
+        features(0, SECOND, h)
+        refresh(0, SECOND, h)
+
         for t in range(PACK):
+            if t + 1 <= LAST:
+                cosine(t + 1, ALL, rest[:])
+                magnitudes(t + 1, ALL)
+                features(t + 1, ALL, weights[t])
             pick(t)
-            if t >= 2:
-                new_rows(t)
-            if t + 1 < PACK:
-                cosine(t + 1, 0, 2)
-                magnitudes(t + 1, 0, 2)
-                features(t + 1, 0, 2, wg[t])
-            if t + 2 < PACK:
-                angles(t + 2, 0, 2)
-                reduce_angles(t + 2, 0, 2, h)
+            if t + 2 <= LAST:
+                angles(t + 2, ALL)
+                rest = h
+                reduce_angles(t + 2, ALL, rest[:])
             if t == 0:
-                quantise_w1(2, 2, 2, nc.scalar.copy)
-                load_page(2)
-                load_wgs(2)
-                load_page(3)
-                load_wgs(3)
-                with nc.allow_non_contiguous_dma(reason="one offset to a partition"):
-                    nc.sync.dma_start(bvec_sb[:], bvec.rearrange("(b p) -> p b", p=P))
+                quantise_w1(2, 2, 2, nc.scalar.copy, rounded_tag="first_features")
+                for later in (2, 3):
+                    load_page(later)
+                    load_weights(later, ALL)
+                with nc.allow_non_contiguous_dma(reason="one value of bvec to a partition and block of rows"):
+                    nc.sync.dma_start(bvec_rows[:], bvec.rearrange("(b p) -> p b", p=P))
             else:
                 reference_rows(t - 1)
-                if t <= 2:
-                    new_rows(t - 1)
-            if t + 1 < PACK:
-                h = wg[t]
-                refresh(t + 1, 0, 2, h)
-        reference_rows(PACK - 1)
+                new_rows(t - 1)
+            if t + 1 <= LAST:
+                h = weights[t]
+                refresh(t + 1, ALL, h)
+        reference_rows(LAST)
+        new_rows(LAST)
 
-        x1_c = keep.tile([P, M], U32, name="x1_c", align_bytes=64)
-        x1_s = keep.tile([P, M], U8, name="x1_s", align_bytes=64)
-        x2_c = keep.tile([P, M], U32, name="x2_c", align_bytes=64)
-        x2_s = keep.tile([P, M], U8, name="x2_s", align_bytes=64)
-        def quantise(codes, scales, rounded, cols):
-            nc.vector.quantize_mx(
-                codes[:, cols].bitcast(E4M3X4), scales[:, cols], rounded[:, cols, :].rearrange("p m t -> p (m t)")
-            )
-
-        halves = pieces(PACK - 1)
-        for cols in halves:
-            quantise(x2_c, x2_s, x2_b, cols)
-            quantise(x1_c, x1_s, x1_b, cols)
-        for pair, hf in ((0, 0), (0, 1), (1, 0), (1, 1)):
-            cols = halves[hf]
-            for b in (2 * pair, 2 * pair + 1):
-                rows = slice(P * b, P * (b + 1))
-                acc = psum.tile([P, M // 2], F32, name="acc_e", tag=(f"result{b}", f"bank{b // 2}_{b % 2}")[hf])
-                nc.tensor.matmul_mx(
-                    acc[:],
-                    lhsT=x1_c[:, rows].bitcast(E4M3X4),
-                    lhsT_scale=x1_s[:, rows],
-                    rhs=x2_c[:, cols].bitcast(E4M3X4),
-                    rhs_scale=x2_s[:, cols],
-                    start=True,
-                    stop=True,
+        x1_codes, x1_plane = held([P, M], U32, "x1_codes"), held([P, M], U8, "x1_plane")
+        x2_codes, x2_plane = held([P, M], U32, "x2_codes"), held([P, M], U8, "x2_plane")
+        for span in (LEFT, RIGHT):
+            for codes, plane, rounded in ((x2_codes, x2_plane, x2_rounded), (x1_codes, x1_plane, x1_rounded)):
+                nc.vector.quantize_mx(
+                    codes[:, span].bitcast(E4M3X4), plane[:, span], rounded[:, span, :].rearrange("p m t -> p (m t)")
                 )
-                res = work.tile([P, M // 2], F32, name="res", bufs=8)
-                if pair == 0 or b % 2 == 0:
-                    nc.scalar.activation(res[:], acc[:], ACT.Identity, bias=bvec_sb[:, b : b + 1])
-                else:
-                    nc.vector.tensor_scalar(res[:], acc[:], bvec_sb[:, b : b + 1], None, ALU.add)
-                nc.sync.dma_start(out[rows, cols], res[:])
+        freed_banks = ("first_angles0", "first_angles1", "sums0", "sums1")
+        for pair in range(2):
+            for span in (LEFT, RIGHT):
+                for b in (2 * pair, 2 * pair + 1):
+                    block = slice(P * b, P * (b + 1))
+                    acc = psum.tile(
+                        [P, M // 2], F32, name="acc_e", tag=f"result{b}" if span.start == 0 else freed_banks[b]
+                    )
+                    nc.tensor.matmul_mx(
+                        acc[:],
+                        lhsT=x1_codes[:, block].bitcast(E4M3X4),
+                        lhsT_scale=x1_plane[:, block],
+                        rhs=x2_codes[:, span].bitcast(E4M3X4),
+                        rhs_scale=x2_plane[:, span],
+                        start=True,
+                        stop=True,
+                    )
+                    result = work.tile([P, M // 2], F32, name="result", bufs=2 * (M // P))
+                    if b < M // P - 1:
+                        nc.scalar.activation(result[:], acc[:], ACT.Identity, bias=bvec_rows[:, b : b + 1])
+                    else:
+                        nc.vector.tensor_scalar(result[:], acc[:], bvec_rows[:, b : b + 1], None, ALU.add)
+                    nc.sync.dma_start(out[block, span], result[:])

import math
from contextlib import ExitStack

import concourse.mybir as mybir

K, H, T, S, T2, M = 1536, 512, 2048, 1024, 2048, 512
FLOPS = 2 * (2 * K * H * S + H * M * M)

F32 = mybir.dt.float32
BF16 = mybir.dt.bfloat16
I32 = mybir.dt.int32
U32 = mybir.dt.uint32
U16 = mybir.dt.uint16
U8 = mybir.dt.uint8
E4M3X4 = mybir.dt.float8_e4m3fn_x4
E2M1X4 = mybir.dt.float4_e2m1fn_x4
ACT = mybir.ActivationFunctionType
ALU = mybir.AluOpType

P = 128
PACK = 4
PASS = P * PACK
PASSES = K // PASS
QUADRANT = 32
QUADRANTS = P // QUADRANT
BLOCKS = 4
PLANE_ROWS = P - QUADRANT + BLOCKS
PER_COLUMN = 16
BANK = 512
FIRST, SECOND, ALL = slice(0, BANK), slice(BANK, S), slice(0, S)
BANK_SPANS = (FIRST, SECOND)
LEFT, RIGHT, BOTH = slice(0, M // 2), slice(M // 2, M), slice(0, M)
LAST = PACK - 1
TWO_PI = 2.0 * math.pi


def entries(offsets, span):
    return offsets[:, span.start // PER_COLUMN : span.stop // PER_COLUMN]


def banks_of(span):
    return range(span.start // BANK, span.stop // BANK)


def tile_list_calciner_batch_likeness_kernel(
    tc, tab_words, tab_scales, offs, offs2, offs3, offs4, w1, w4_words, w4_scales, wgs, page0, mu, gain, bvec, out
):
    nc = tc.nc
    with ExitStack() as ctx:
        lists = ctx.enter_context(tc.tile_pool(name="lists", bufs=1))
        keep = ctx.enter_context(tc.tile_pool(name="keep", bufs=1))
        work = ctx.enter_context(tc.tile_pool(name="work", bufs=2))
        psum = ctx.enter_context(tc.psum_pool(name="psum", bufs=1))

        def held(shape, dtype, name, tag=None):
            return keep.tile(shape, dtype, name=name, tag=tag or name, align_bytes=64)

        idx = lists.tile([P, S // PER_COLUMN], U16, name="idx")
        idx2 = lists.tile([P, S // PER_COLUMN], U16, name="idx2")
        idx3 = lists.tile([P, M // PER_COLUMN], U16, name="idx3")
        idx4 = lists.tile([P, M // PER_COLUMN], U16, name="idx4")

        table_scales = held([P, T], U8, "table_scales")
        w4_scales_raw = held([P, PASSES, H], U8, "w4_scales_raw")
        moved_planes = [held([P, S], U8, f"moved_plane{a}") for a in range(1, PASSES)]
        nc.vector.memset(table_scales[:].bitcast(I32), 0)
        nc.vector.memset(w4_scales_raw[:].rearrange("p a c -> p (a c)").bitcast(I32), 0)
        for plane in moved_planes:
            nc.vector.memset(plane[:].bitcast(I32), 0)

        warm = keep.tile([P, 2], F32, name="warm")
        nc.gpsimd.memset(warm[:, 0:1], 0.0)
        nc.scalar.activation(warm[:, 1:2], warm[:, 0:1], ACT.Sin)

        w1_raw, table_words, weights, page = {}, {}, {}, {}
        wgs_rows = wgs.rearrange("(q t) s -> t q s", t=PACK)
        page_rows = page0.rearrange("(p t) c -> t p c", t=PACK)

        def load_w1(a):
            w1_raw[a] = held([P, PACK, H], F32, f"w1_raw{a}")
            nc.sync.dma_start(w1_raw[a][:], w1[PASS * a : PASS * (a + 1), :].rearrange("(p j) c -> p j c", j=PACK))

        def load_table(a):
            table_words[a] = held([P, T], I32, f"table_words{a}")
            nc.sync.dma_start(table_words[a][:], tab_words[a].rearrange("p t i -> p (t i)").bitcast(I32))

        def load_page(t):
            page[t] = held([P, T2], F32, f"page{t}")
            nc.sync.dma_start(page[t][:], page_rows[t])

        def load_weights(t, span):
            if span.start == 0:
                weights[t] = held([P, S], F32, f"weights{t}")
            for q in (0, 2, 1, 3):
                nc.sync.dma_start(weights[t][QUADRANT * q : QUADRANT * (q + 1), span], wgs_rows[t][:, span])

        w4_raw = held([P, PASSES, 2 * H], U8, "w4_raw")
        nc.sync.dma_start(idx[:], offs)
        nc.sync.dma_start(w4_raw[:].bitcast(I32), w4_words.rearrange("a p n -> p a n").bitcast(I32))
        load_table(0)
        for q in range(QUADRANTS):
            nc.sync.dma_start(
                table_scales[QUADRANT * q : QUADRANT * q + BLOCKS * PASSES, :].bitcast(I32),
                tab_scales[:, BLOCKS * q : BLOCKS * (q + 1), :].bitcast(I32),
            )
        load_w1(0)
        for q in range(QUADRANTS):
            nc.sync.dma_start(
                w4_scales_raw[QUADRANT * q : QUADRANT * q + BLOCKS, :, :].bitcast(I32),
                w4_scales[:, BLOCKS * q : BLOCKS * (q + 1), :].rearrange("a r c -> r a c").bitcast(I32),
            )
        load_table(1)
        load_w1(1)
        load_table(2)

        w4_codes = held([P, PASSES, PACK, P], U16, "w4_codes")
        w4_planes = held([P, PASSES, PACK, P], U8, "w4_planes")
        nc.vector.tensor_copy(w4_codes[:], w4_raw[:].bitcast(U16).rearrange("p a (q t) -> p a t q", t=PACK))

        picked_scales = held([P, S], U8, "picked_scales")
        nc.vector.tensor_copy(picked_scales[:], table_scales[:].indirect(idx[:]))
        for a in range(1, PASSES):
            nc.sync.dma_start(
                moved_planes[a - 1][0:PLANE_ROWS, :].bitcast(I32),
                picked_scales[BLOCKS * a : BLOCKS * a + PLANE_ROWS, :].bitcast(I32),
            )
        planes_for_w4 = [picked_scales] + moved_planes
        planes_for_w1 = [picked_scales[BLOCKS * a :, :] for a in range(PASSES)]
        load_w1(2)
        nc.sync.dma_start(idx2[:], offs2)
        load_weights(0, FIRST)
        nc.vector.tensor_copy(w4_planes[:], w4_scales_raw[:].rearrange("p a (q t) -> p a t q", t=PACK))

        picked_words = {}
        for a in range(PASSES):
            for n, span in enumerate(BANK_SPANS):
                picked_words[a, n] = held([P, BANK], U32, f"picked_words{a}_{n}")
                nc.vector.tensor_copy(
                    picked_words[a, n][:], table_words[a][:].bitcast(U32).indirect(entries(idx, span))
                )

        mu_rows = keep.tile([P, PACK], F32, name="mu_rows")
        gain_rows = keep.tile([P, PACK], F32, name="gain_rows")
        minus_mu = keep.tile([P, PACK], F32, name="minus_mu")
        bvec_rows = keep.tile([P, M // P], F32, name="bvec_rows")
        load_page(0)
        load_weights(0, SECOND)
        nc.sync.dma_start(idx4[:], offs4)
        nc.sync.dma_start(idx3[:], offs3)
        nc.sync.dma_start(mu_rows[:], mu.rearrange("(p t) -> p t", t=PACK))
        nc.sync.dma_start(gain_rows[:], gain.rearrange("(p t) -> p t", t=PACK))
        nc.scalar.activation(minus_mu[:], mu_rows[:], ACT.Copy, scale=-1.0)

        w1_codes, w1_planes = {}, {}

        def quantise_w1(a, t0, count, copy, rounded_tag=None, codes_tag=None):
            rounded = held([P, count, P, PACK], BF16, f"w1_rounded{a}_{t0}", rounded_tag)
            source = w1_raw[a][:].rearrange("p j (q t) -> p q j t", t=PACK)[:, :, :, t0 : t0 + count]
            copy(rounded[:].rearrange("p t q j -> p q j t"), source)
            codes = held([P, count, P], U32, f"w1_codes{a}_{t0}", codes_tag)
            scales = held([P, count, P], U8, f"w1_planes{a}_{t0}")
            nc.vector.quantize_mx(
                codes[:].rearrange("p t q -> p (t q)").bitcast(E4M3X4),
                scales[:].rearrange("p t q -> p (t q)"),
                rounded[:].rearrange("p t q j -> p (t q j)"),
            )
            for t in range(count):
                w1_codes[a, t0 + t] = codes[:, t, :]
                w1_planes[a, t0 + t] = scales[:, t, :]

        for a in range(PASSES - 1):
            quantise_w1(a, 0, PACK, nc.scalar.copy, codes_tag=f"table_words{a + 1}")
        quantise_w1(2, 0, 2, nc.vector.tensor_copy, rounded_tag="late_rounded")
        load_weights(1, ALL)
        load_page(1)

        rows = {}

        def row_tile(name, t, dtype=F32):
            if (name, t) not in rows:
                rows[name, t] = work.tile([P, S], dtype, name=name)
            return rows[name, t]

        def product(acc, codes, scales, table_planes, n):
            for a in range(PASSES):
                nc.tensor.matmul_mx(
                    acc[:],
                    lhsT=codes[a],
                    lhsT_scale=scales[a],
                    rhs=picked_words[a, n][:].bitcast(E4M3X4),
                    rhs_scale=table_planes[a][:, BANK_SPANS[n]],
                    start=(a == 0),
                    stop=(a == PASSES - 1),
                )

        def angles(t, span):
            for n in banks_of(span):
                acc = psum.tile([P, BANK], F32, name="acc_b", tag=f"first_angles{n}" if t == 0 else f"sums{n}")
                codes = [w4_codes[:, a, t, :].bitcast(E2M1X4) for a in range(PASSES)]
                product(acc, codes, [w4_planes[:, a, t, :] for a in range(PASSES)], planes_for_w4, n)
                nc.scalar.activation(row_tile("abs_b", t)[:, BANK_SPANS[n]], acc[:], ACT.Abs)
                nc.scalar.activation(row_tile("turns", t, U32)[:, BANK_SPANS[n]], acc[:], ACT.Abs, scale=1.0 / TWO_PI)

        def reduce_angles(t, span, rest):
            turns = row_tile("turns", t, U32)[:, span].bitcast(I32)
            nc.vector.scalar_tensor_tensor(rest, turns, -TWO_PI, row_tile("abs_b", t)[:, span], ALU.mult, ALU.add)

        def cosine(t, span, rest):
            folded = work.tile([P, span.stop - span.start], F32, name="folded", bufs=1)
            nc.scalar.activation(folded[:], rest, ACT.Abs)
            nc.scalar.activation(row_tile("cos_b", t)[:, span], folded[:], ACT.Sin, bias=math.pi / 2, scale=-1.0)

        def magnitudes(t, span):
            for n in banks_of(span):
                acc = psum.tile([P, BANK], F32, name="acc_a", tag=f"sums{n}")
                codes = [w1_codes[a, t].bitcast(E4M3X4) for a in range(PASSES)]
                product(acc, codes, [w1_planes[a, t] for a in range(PASSES)], planes_for_w1, n)
                nc.scalar.activation(row_tile("abs_a", t)[:, BANK_SPANS[n]], acc[:], ACT.Abs)

        def features(t, span, h):
            nc.vector.tensor_tensor(h[:, span], row_tile("abs_a", t)[:, span], row_tile("cos_b", t)[:, span], ALU.mult)

        def refresh(t, span, h):
            nc.vector.tensor_tensor(page[t][:].indirect(entries(idx2, span)), h[:, span], weights[t][:, span], ALU.mult)

        x1_rounded = held([P, M, PACK], BF16, "x1_rounded")
        x2_rounded = held([P, M, PACK], BF16, "x2_rounded")
        picked_ref, picked_new = {}, {}
        picks_alive = 6

        def spans_of(t):
            return (LEFT, RIGHT) if t == LAST else (BOTH,)

        def pick(t):
            for picked, offsets in ((picked_ref, idx4), (picked_new, idx3)):
                picked[t] = work.tile([P, M], F32, name="picked", bufs=picks_alive)
                for span in spans_of(t):
                    nc.vector.tensor_copy(picked[t][:, span], page[t][:].indirect(entries(offsets, span)))

        def reference_rows(t):
            abs_ref = work.tile([P, M], F32, name="abs_ref")
            for span in spans_of(t):
                nc.scalar.activation(abs_ref[:, span], picked_ref[t][:, span], ACT.Abs)
                nc.scalar.activation(x2_rounded[:, span, t], abs_ref[:, span], ACT.Copy, scale=gain_rows[:, t : t + 1])

        last_pair = held([P, 2, M], BF16, "last_pair")

        def new_rows(t):
            shift = minus_mu[:, t : t + 1]
            if t < LAST:
                rounded = x1_rounded[:, :, t] if t < 2 else last_pair[:, 0, :]
                nc.scalar.activation(rounded, picked_new[t][:], ACT.Identity, bias=shift)
            else:
                for span in spans_of(t):
                    nc.vector.tensor_scalar(last_pair[:, 1, span], picked_new[t][:, span], shift, None, ALU.add)
                for span in spans_of(t):
                    pair_by_column = last_pair[:, :, span].rearrange("p t m -> p m t")
                    nc.vector.tensor_copy(x1_rounded[:, span, 2:PACK], pair_by_column)

        rest_first = held([P, BANK], F32, "rest_first")
        rest_second = held([P, BANK], F32, "rest_second", "late_rounded")
        h = held([P, S], F32, "first_features")
        angles(0, FIRST)
        reduce_angles(0, FIRST, rest_first[:])
        angles(0, SECOND)
        reduce_angles(0, SECOND, rest_second[:])
        cosine(0, FIRST, rest_first[:])
        magnitudes(0, FIRST)
        features(0, FIRST, h)
        refresh(0, FIRST, h)
        cosine(0, SECOND, rest_second[:])
        magnitudes(0, SECOND)
        angles(1, ALL)
        rest = h
        reduce_angles(1, ALL, rest[:])
        h = row_tile("abs_b", 1)
        features(0, SECOND, h)
        refresh(0, SECOND, h)

        for t in range(PACK):
            if t + 1 <= LAST:
                cosine(t + 1, ALL, rest[:])
                magnitudes(t + 1, ALL)
                features(t + 1, ALL, weights[t])
            pick(t)
            if t + 2 <= LAST:
                angles(t + 2, ALL)
                rest = h
                reduce_angles(t + 2, ALL, rest[:])
            if t == 0:
                quantise_w1(2, 2, 2, nc.scalar.copy, rounded_tag="first_features")
                for later in (2, 3):
                    load_page(later)
                    load_weights(later, ALL)
                with nc.allow_non_contiguous_dma(reason="one value of bvec to a partition and block of rows"):
                    nc.sync.dma_start(bvec_rows[:], bvec.rearrange("(b p) -> p b", p=P))
            else:
                reference_rows(t - 1)
                new_rows(t - 1)
            if t + 1 <= LAST:
                h = weights[t]
                refresh(t + 1, ALL, h)
        reference_rows(LAST)
        new_rows(LAST)

        x1_codes, x1_plane = held([P, M], U32, "x1_codes"), held([P, M], U8, "x1_plane")
        x2_codes, x2_plane = held([P, M], U32, "x2_codes"), held([P, M], U8, "x2_plane")
        for span in (LEFT, RIGHT):
            for codes, plane, rounded in ((x2_codes, x2_plane, x2_rounded), (x1_codes, x1_plane, x1_rounded)):
                nc.vector.quantize_mx(
                    codes[:, span].bitcast(E4M3X4), plane[:, span], rounded[:, span, :].rearrange("p m t -> p (m t)")
                )
        freed_banks = ("first_angles0", "first_angles1", "sums0", "sums1")
        for pair in range(2):
            for span in (LEFT, RIGHT):
                for b in (2 * pair, 2 * pair + 1):
                    block = slice(P * b, P * (b + 1))
                    acc = psum.tile(
                        [P, M // 2], F32, name="acc_e", tag=f"result{b}" if span.start == 0 else freed_banks[b]
                    )
                    nc.tensor.matmul_mx(
                        acc[:],
                        lhsT=x1_codes[:, block].bitcast(E4M3X4),
                        lhsT_scale=x1_plane[:, block],
                        rhs=x2_codes[:, span].bitcast(E4M3X4),
                        rhs_scale=x2_plane[:, span],
                        start=True,
                        stop=True,
                    )
                    result = work.tile([P, M // 2], F32, name="result", bufs=2 * (M // P))
                    if b < M // P - 1:
                        nc.scalar.activation(result[:], acc[:], ACT.Identity, bias=bvec_rows[:, b : b + 1])
                    else:
                        nc.vector.tensor_scalar(result[:], acc[:], bvec_rows[:, b : b + 1], None, ALU.add)
                    nc.sync.dma_start(out[block, span], result[:])
